import numpy as np
import ml_dtypes


def mxq(x, axis, fmt="e4m3"):
    dtype, down = {"e4m3": (ml_dtypes.float8_e4m3fn, 7), "e5m2": (ml_dtypes.float8_e5m2, 14)}[fmt]
    v = np.moveaxis(np.asarray(x, np.float32).astype(ml_dtypes.bfloat16).astype(np.float64), axis, -1)
    blocks = v.reshape(v.shape[:-1] + (-1, 32))
    amax = np.abs(blocks).max(-1, keepdims=True)
    byte = np.maximum(np.where(amax > 0, np.frexp(amax)[1] - 1 + 127, 0) - down, 1)
    scale = np.exp2(byte - 127.0)
    codes = (blocks / scale).astype(np.float32).astype(dtype).astype(np.float64)
    return np.moveaxis((codes * scale).reshape(v.shape), -1, axis)


WIDE = False


def mx_kscale(k):
    if not WIDE:
        return np.ones(k)
    levels = np.array([10, -10, 5, -5, 0])
    if k % 512:
        return np.exp2(np.random.permutation(np.resize(levels, k // 32))).repeat(32)
    a = np.empty((k // 512, 16))
    for p in range(k // 512):
        a[p, :8] = np.random.permutation(np.resize(levels, 8))
        for g in range(8):
            far = levels[np.abs(levels - a[p, g]) >= 10]
            a[p, g + 8] = far[np.random.randint(len(far))]
    return np.exp2(a.ravel()).repeat(32)


BF16 = ml_dtypes.bfloat16


def bf(x):
    return np.asarray(x, np.float32).astype(BF16)


def f64(x):
    return np.asarray(x).astype(np.float64)


E2M1 = np.array([0.0, 0.5, 1.0, 1.5, 2.0, 3.0, 4.0, 6.0, -0.0, -0.5, -1.0, -1.5, -2.0, -3.0, -4.0, -6.0])


def pack_weight(w, fmt):
    k, n = w.shape
    w = f64(bf(w)).reshape(k // 32, 32, n)
    amax = np.abs(w).max(1)
    if fmt == "e4m3":
        byte = np.frexp(amax)[1] - 1 + 127 - 7
    else:
        mant, ex = np.frexp(amax / 6.0)
        byte = np.where(mant > 0.5, ex, ex - 1) + 127
    byte = np.clip(np.where(amax > 0, byte, 1), 1, 254)
    scaled = (w * np.exp2(127.0 - byte)[:, None, :]).reshape(k, n).astype(np.float32)
    by_word = np.ascontiguousarray(scaled.reshape(k // 512, 128, 4, n).transpose(0, 1, 3, 2))
    if fmt == "e4m3":
        words = by_word.astype(ml_dtypes.float8_e4m3fn).view(np.uint8)
    else:
        c = by_word.astype(ml_dtypes.float4_e2m1fn).view(np.uint8) & 0xF
        words = c[..., 0::2] | (c[..., 1::2] << 4)
    return np.ascontiguousarray(words), np.ascontiguousarray(byte.astype(np.uint8).reshape(k // 512, 16, n))


def unpack_weight(words, scales, fmt):
    g, p, n, _ = words.shape
    if fmt == "e4m3":
        vals = np.ascontiguousarray(words).view(ml_dtypes.float8_e4m3fn).astype(np.float64)
    else:
        nib = np.empty((g, p, n, 4), np.uint8)
        nib[..., 0::2] = words & 0xF
        nib[..., 1::2] = words >> 4
        vals = E2M1[nib]
    vals = vals * np.repeat(np.exp2(scales.astype(np.float64) - 127.0), 8, axis=1)[..., None]
    return vals.transpose(0, 1, 3, 2).reshape(g * 512, n)
def pack4(w):
    words, scales = pack_weight(w, "e2m1")
    return words.reshape(words.shape[0], 128, -1), scales


def unpack4(words, scales):
    return unpack_weight(words.reshape(words.shape[0], 128, -1, 2), scales, "e2m1")


L, K, R, N, C = 1024, 2048, 1024, 1024, 2


def setup_inputs():
    s, t, v = mx_kscale(K), mx_kscale(R), mx_kscale(R)
    x = np.random.standard_normal((L, K)) * s
    comp = np.random.standard_normal((K, R)) / np.sqrt(K) / s[:, None] * t
    a = np.random.standard_normal((R, R)) / np.sqrt(R) * v[:, None] / t
    d = 4 * np.random.standard_normal((R, N)) / np.sqrt(R) / v[:, None]
    a_words, a_scales = pack4(a)
    d_words, d_scales = pack4(d)
    return {"x": bf(x),
            "comp": bf(comp),
            "gain": bf(1 + 0.1 * np.random.standard_normal(R)),
            "a_words": a_words, "a_scales": a_scales,
            "d_words": d_words, "d_scales": d_scales,
            "copy_gain": bf(1 + 0.1 * np.random.standard_normal((C, N))),
            "base": bf(np.random.standard_normal((L, C * N)))}


def reference(x, comp, gain, a_words, a_scales, d_words, d_scales, copy_gain, base):
    z = (mxq(f64(x), 1, "e4m3") @ mxq(f64(comp), 0, "e4m3")) * f64(gain)
    e = unpack4(a_words, a_scales).T @ unpack4(d_words, d_scales)
    y = mxq(z, 1, "e4m3") @ mxq(e, 0, "e4m3")
    out = f64(base).reshape(L, C, N) + y[:, None, :] * f64(copy_gain)
    return out.reshape(L, C * N)

@@ -1,0 +1,422 @@
+from contextlib import ExitStack
+
+import concourse.mybir as mybir
+from concourse.masks import make_identity
+
+F32 = mybir.dt.float32
+BF16 = mybir.dt.bfloat16
+I32 = mybir.dt.int32
+U32 = mybir.dt.uint32
+U8 = mybir.dt.uint8
+FP8 = mybir.dt.float8_e4m3fn_x4
+FP4 = mybir.dt.float4_e2m1fn_x4
+ADD = mybir.AluOpType.add
+MULT = mybir.AluOpType.mult
+COPY = mybir.ActivationFunctionType.Copy
+
+L, K, R, N, C = 1024, 2048, 1024, 1024, 2
+FLOPS = 2 * L * K * R + 2 * R * R * N + 2 * L * R * N
+
+P = 128
+KG = K // 512
+RT = R // 512
+PAIRS = L // 256
+SLICE_ENGINE = ("vvvs", "vvvs", "vvvs", "vvvs")
+TR_PAIRS = (2, 3)
+G_ADD = {(i, jh) for i in range(8) for jh in range(2) if (jh == 0 and i < 7) or i in (1, 3)}
+MANUAL = True
+
+
+def tile_mora_repeated_update_s12_kernel(tc, x, comp, gain, a_words, a_scales, d_words, d_scales, copy_gain, base, out):
+    nc = tc.nc
+    with ExitStack() as ctx:
+        one = ctx.enter_context(tc.tile_pool(name="one", bufs=1))
+        sb = ctx.enter_context(tc.tile_pool(name="sb", bufs=2))
+        ps = ctx.enter_context(tc.psum_pool(name="ps", bufs=2))
+        if MANUAL:
+            ctx.enter_context(tc.manual_schedule())
+
+        a_raw = one.tile([P, 2, 2048], U8, name="a_raw", align_bytes=64)
+        a_perm = one.tile([P, 2, 2048], U8, name="a_perm", align_bytes=64)
+        d_raw = one.tile([P, 2, 2048], U8, name="d_raw", align_bytes=64)
+        as_raw = one.tile([P, 2, 1024], U8, name="as_raw", align_bytes=64)
+        as_perm = one.tile([P, 2, 1024], U8, name="as_perm", align_bytes=64)
+        ds_raw = one.tile([P, 2, 1024], U8, name="ds_raw", align_bytes=64)
+        comp_codes = one.tile([P, KG, R], U32, name="comp_codes", align_bytes=64)
+        comp_scales = one.tile([P, KG, R], U8, name="comp_scales", align_bytes=64)
+        e_codes = one.tile([P, RT, N], U32, name="e_codes", align_bytes=64)
+        e_scales = one.tile([P, RT, N], U8, name="e_scales", align_bytes=64)
+        cg = one.tile([P, C, N], BF16, name="cg", align_bytes=64)
+        ident = one.tile([P, P], F32, name="ident", align_bytes=64)
+        gain_rows = one.tile([16, P], BF16, name="gain_rows", align_bytes=64)
+        gain_sq = one.tile([P, P], F32, name="gain_sq", align_bytes=64)
+        gain_col = one.tile([P, 16], F32, name="gain_col", align_bytes=64)
+        warm = one.tile([P, 1], F32, name="warm", align_bytes=64)
+
+        nc.vector.memset(as_raw[:].rearrange("p g n -> p (g n)").bitcast(I32), 0)
+        nc.vector.memset(ds_raw[:].rearrange("p g n -> p (g n)").bitcast(I32), 0)
+        nc.vector.memset(warm[:], 0.0)
+        nc.vector.memset(gain_sq[:], 0.0)
+        make_identity(nc, ident[:])
+
+        for t in range(RT):
+            nc.scalar.dma_start(
+                out=gain_rows[4 * t : 4 * t + 4, :].rearrange("t (q e) -> t q e", e=8),
+                in_=gain[512 * t : 512 * (t + 1)].rearrange("(q t e) -> t q e", t=4, e=8),
+            )
+        for c in range(C):
+            nc.scalar.dma_start(
+                out=gain_rows[8 + 4 * c : 12 + 4 * c, :],
+                in_=copy_gain[c, 512:1024].rearrange("(b p) -> b p", p=P),
+            )
+        nc.scalar.activation(out=warm[:], in_=warm[:], func=COPY)
+
+        x_tiles = {}
+        comp_raw = {}
+        base_tiles = {}
+
+        def load_x(i):
+            xt = sb.tile([P, K], BF16, name="x_in", bufs=4, align_bytes=64)
+            nc.sync.dma_start(out=xt[:], in_=x[P * i : P * (i + 1), :])
+            x_tiles[i] = xt
+
+        def load_comp(g, rt):
+            ct = sb.tile([P, 4, 512], BF16, name="comp_raw", bufs=5, align_bytes=64)
+            nc.sync.dma_start(
+                out=ct[:],
+                in_=comp[512 * g : 512 * (g + 1), 512 * rt : 512 * (rt + 1)].rearrange("(p j) r -> p j r", j=4),
+            )
+            comp_raw[(g, rt)] = ct
+
+        def load_base(i):
+            bt = sb.tile([P, C, N], BF16, name="base_in", bufs=4, align_bytes=64)
+            nc.sync.dma_start(out=bt[:].rearrange("p c n -> p (c n)"), in_=base[P * i : P * (i + 1), :])
+            base_tiles[i] = bt
+
+        nc.sync.dma_start(out=a_raw[:].bitcast(I32), in_=a_words.rearrange("g p n -> p g n").bitcast(I32))
+        for raw, src in ((as_raw, a_scales), (ds_raw, d_scales)):
+            for q in range(4):
+                nc.sync.dma_start(
+                    out=raw[32 * q : 32 * q + 4, :, :].bitcast(I32),
+                    in_=src[:, 4 * q : 4 * q + 4, :].rearrange("g r n -> r g n").bitcast(I32),
+                )
+        nc.sync.dma_start(out=d_raw[:].bitcast(I32), in_=d_words.rearrange("g p n -> p g n").bitcast(I32))
+        load_comp(0, 0)
+        load_x(0)
+        load_comp(1, 0)
+        load_x(1)
+        load_comp(2, 0)
+        load_comp(3, 0)
+        load_x(2)
+        load_x(3)
+        for g in range(KG):
+            load_comp(g, 1)
+        load_x(4)
+        load_x(5)
+        nc.sync.dma_start(out=cg[:].rearrange("p c n -> p (c n)"), in_=copy_gain.rearrange("c n -> (c n)").partition_broadcast(P))
+        load_base(0)
+        load_base(1)
+
+        xg_tiles = {}
+        x_codes = {}
+
+        def x_transpose(i):
+            s, h = divmod(i, 2)
+            if h == 0:
+                xg_tiles[s] = sb.tile([P, KG, 256, 2], F32, name="xg", align_bytes=64)
+            words = x_tiles[i][:].bitcast(F32)
+            for b in range(2):
+                bank = ps.tile([P, 4, P], F32, name="xt_ps", bufs=2)
+                for g2 in range(2):
+                    for u in range(2):
+                        w0 = 256 * (2 * b + g2) + u
+                        nc.tensor.transpose(bank[:, 2 * g2 + u, :], words[:, w0 : w0 + 255 : 2], ident[:])
+                nc.scalar.copy(
+                    out=xg_tiles[s][:, 2 * b : 2 * b + 2, P * h : P * (h + 1), :],
+                    in_=bank[:].rearrange("p (g u) r -> p g r u", u=2),
+                )
+
+        def x_quant(s):
+            codes = sb.tile([P, KG, 256], U32, name="x_codes", bufs=3, align_bytes=64)
+            scales = sb.tile([P, KG, 256], U8, name="x_scales", bufs=3, align_bytes=64)
+            nc.vector.quantize_mx(
+                out=codes[:].rearrange("p g r -> p (g r)").bitcast(FP8),
+                scales=scales[:].rearrange("p g r -> p (g r)"),
+                in_=xg_tiles[s][:].rearrange("p g r u -> p (g r u)").bitcast(BF16),
+            )
+            x_codes[s] = (codes, scales)
+
+        comp_grouped = {}
+
+        def comp_group(g, rt, t0, t1, eng):
+            key = (g, rt)
+            if key not in comp_grouped:
+                comp_grouped[key] = sb.tile([P, 4, 16, 8, 4], BF16, name="comp_grouped", bufs=3, align_bytes=64)
+            dst = comp_grouped[key][:, t0:t1, :, :, :]
+            src = comp_raw[key][:].rearrange("p j (q t e) -> p t q e j", t=4, e=8)[:, t0:t1, :, :, :]
+            if t1 - t0 == 1:
+                dst = dst.rearrange("p t q e j -> p (t q) e j")
+                src = comp_raw[key][:].rearrange("p j (q t e) -> p t q e j", t=4, e=8)[:, t0, :, :, :]
+            if eng == "v":
+                nc.vector.tensor_copy(out=dst, in_=src)
+            else:
+                nc.scalar.copy(out=dst, in_=src)
+
+        def comp_quant(g, rt):
+            cols = slice(512 * rt, 512 * (rt + 1))
+            nc.vector.quantize_mx(
+                out=comp_codes[:, g, cols].bitcast(FP8),
+                scales=comp_scales[:, g, cols],
+                in_=comp_grouped[(g, rt)][:].rearrange("p t q e j -> p (t q e j)"),
+            )
+
+        eg_tiles = {}
+
+        def e_block(rt, nb):
+            bank = ps.tile([P, 4, P], F32, name="acc_ps", bufs=4)
+            for t in range(4):
+                col = 512 * rt + 128 * t
+                for g in range(2):
+                    nc.tensor.matmul_mx(
+                        out=bank[:, t, :],
+                        lhsT=a_perm[:, g, 2 * col : 2 * col + 256].bitcast(FP4),
+                        lhsT_scale=as_perm[:, g, col : col + 128],
+                        rhs=d_raw[:, g, 256 * nb : 256 * (nb + 1)].bitcast(FP4),
+                        rhs_scale=ds_raw[:, g, 128 * nb : 128 * (nb + 1)],
+                        start=(g == 0),
+                        stop=(g == 1),
+                    )
+            key = (rt, nb // 4)
+            if nb % 4 == 0:
+                eg_tiles[key] = sb.tile([P, 512, 4], BF16, name="eg", bufs=4, align_bytes=64)
+            c0 = 128 * (nb % 4)
+            nc.scalar.copy(out=eg_tiles[key][:, c0 : c0 + 128, :], in_=bank[:].rearrange("p t n -> p n t"))
+
+        def e_quant(rt, jh):
+            nc.vector.quantize_mx(
+                out=e_codes[:, rt, 512 * jh : 512 * (jh + 1)].bitcast(FP8),
+                scales=e_scales[:, rt, 512 * jh : 512 * (jh + 1)],
+                in_=eg_tiles[(rt, jh)][:].rearrange("p n t -> p (n t)"),
+            )
+
+        zc_tiles = {}
+        zg_tiles = {}
+        z_codes = {}
+
+        def z_bank(s, rt, th):
+            codes, scales = x_codes[s]
+            if th == 0:
+                zc_tiles[(s, rt)] = sb.tile([P, 4, 256], BF16, name="zc", bufs=3, align_bytes=64)
+            zc = zc_tiles[(s, rt)]
+            bank = ps.tile([P, 2, 256], F32, name="acc_ps", bufs=4)
+            for h in range(2):
+                col = 512 * rt + 128 * (2 * th + h)
+                for g in range(KG):
+                    nc.tensor.matmul_mx(
+                        out=bank[:, h, :],
+                        lhsT=comp_codes[:, g, col : col + 128].bitcast(FP8),
+                        lhsT_scale=comp_scales[:, g, col : col + 128],
+                        rhs=codes[:, g, :].bitcast(FP8),
+                        rhs_scale=scales[:, g, :],
+                        start=(g == 0),
+                        stop=(g == KG - 1),
+                    )
+            for h in range(2):
+                t = 2 * th + h
+                nc.scalar.activation(out=zc[:, t, :], in_=bank[:, h, :], func=COPY, scale=gain_col[:, 4 * rt + t : 4 * rt + t + 1])
+
+        def z_group(s, rt):
+            zg = sb.tile([P, 256, 4], BF16, name="zg", bufs=4, align_bytes=64)
+            nc.scalar.copy(out=zg[:], in_=zc_tiles[(s, rt)][:].rearrange("p t r -> p r t"))
+            zg_tiles[(s, rt)] = zg
+
+        def z_quant(s, rt):
+            codes = sb.tile([P, 256], U32, name="z_codes", bufs=8, align_bytes=64)
+            scales = sb.tile([P, 256], U8, name="z_scales", bufs=8, align_bytes=64)
+            nc.vector.quantize_mx(out=codes[:].bitcast(FP8), scales=scales[:], in_=zg_tiles[(s, rt)][:].rearrange("p r t -> p (r t)"))
+            z_codes[(s, rt)] = (codes, scales)
+
+        y_banks = {}
+        out_tiles = {}
+
+
+        def col_range(jh):
+            return slice(512 * jh, 512 * (jh + 1))
+
+        def y_matmul(i, jh):
+            s, h = divmod(i, 2)
+            cols = col_range(jh)
+            width = cols.stop - cols.start
+            bank = ps.tile([P, width], F32, name="y_ps", tag="y_ps", bufs=2)
+            for rt in range(RT):
+                codes, scales = z_codes[(s, rt)]
+                nc.tensor.matmul_mx(
+                    out=bank[:],
+                    lhsT=codes[:, P * h : P * (h + 1)].bitcast(FP8),
+                    lhsT_scale=scales[:, P * h : P * (h + 1)],
+                    rhs=e_codes[:, rt, cols].bitcast(FP8),
+                    rhs_scale=e_scales[:, rt, cols],
+                    start=(rt == 0),
+                    stop=(rt == RT - 1),
+                )
+            y_banks[(i, jh)] = bank
+
+        def y_mult(i, jh):
+            cols = col_range(jh)
+            width = cols.stop - cols.start
+            out_tiles[(i, jh)] = sb.tile([P, C, width], F32, name="out_sb", tag=f"out_sb{jh}", bufs=4 - 2 * jh, align_bytes=64)
+            nc.vector.tensor_tensor(
+                out=out_tiles[(i, jh)][:],
+                in0=y_banks[(i, jh)][:].unsqueeze(1).to_broadcast([P, C, width]),
+                in1=cg[:, :, cols],
+                op=MULT,
+            )
+
+        def y_add(i, jh):
+            cols = col_range(jh)
+            eng = nc.gpsimd if (i, jh) in G_ADD else nc.vector
+            ot = out_tiles[(i, jh)]
+            eng.tensor_tensor(out=ot[:], in0=ot[:], in1=base_tiles[i][:, :, cols], op=ADD)
+            store(i, cols, ot)
+
+        yt_tiles = {}
+
+        def yt_matmul(s):
+            yt = sb.tile([P, C, 4, 256], F32, name="yt", bufs=1, align_bytes=64)
+            yt_banks = []
+            for bb in range(2):
+                bank = ps.tile([P, 2, 256], F32, name="acc_ps", bufs=4)
+                for b2 in range(2):
+                    cols = slice(512 + P * (2 * bb + b2), 512 + P * (2 * bb + b2 + 1))
+                    for rt in range(RT):
+                        codes, scales = z_codes[(s, rt)]
+                        nc.tensor.matmul_mx(
+                            out=bank[:, b2, :],
+                            lhsT=e_codes[:, rt, cols].bitcast(FP8),
+                            lhsT_scale=e_scales[:, rt, cols],
+                            rhs=codes[:].bitcast(FP8),
+                            rhs_scale=scales[:],
+                            start=(rt == 0),
+                            stop=(rt == RT - 1),
+                        )
+                yt_banks.append(bank)
+            for c in range(C):
+                for b in range(4):
+                    k = 8 + 4 * c + b
+                    nc.scalar.activation(out=yt[:, c, b, :], in_=yt_banks[b // 2][:, b % 2, :], func=COPY, scale=gain_col[:, k : k + 1])
+            yt_tiles[s] = yt
+
+        def yt_back(i, c):
+            s, h = divmod(i, 2)
+            bank = ps.tile([P, 4, P], F32, name="xt_ps", bufs=2)
+            for b in range(4):
+                nc.tensor.transpose(bank[:, b, :], yt_tiles[s][:, c, b, P * h : P * (h + 1)], ident[:])
+            ot = sb.tile([P, 512], F32, name="out_sb", tag="out_tr", bufs=6, align_bytes=64)
+            nc.vector.tensor_tensor(out=ot[:], in0=bank[:].rearrange("p b t -> p (b t)"), in1=base_tiles[i][:, c, 512:1024], op=ADD)
+            nc.sync.dma_start(out=out[P * i : P * (i + 1), N * c + 512 : N * (c + 1)], in_=ot[:])
+
+        def store(i, cols, ot):
+            nc.sync.dma_start(out=out[P * i : P * (i + 1), :].rearrange("p (c n) -> p c n", c=C)[:, :, cols], in_=ot[:])
+
+        def a_permute(dst, raw, g, w):
+            nc.vector.tensor_copy(
+                out=dst[:, g, :].bitcast(I32).rearrange("p (r t q w) -> p r t q w", r=2, t=4, w=w),
+                in_=raw[:, g, :].bitcast(I32).rearrange("p (r q t w) -> p r t q w", r=2, t=4, w=w),
+            )
+
+        order = [(rt, jh) for jh in range(2) for rt in range(2)]
+        for g in range(2):
+            a_permute(a_perm, a_raw, g, 4)
+            a_permute(as_perm, as_raw, g, 2)
+
+        def comp_piece(g, rt):
+            comp_group(g, rt, 0, 4, "v")
+            comp_quant(g, rt)
+
+        def e_quarter(n):
+            rt, jh = order[n]
+            for nb in range(4):
+                e_block(rt, 4 * jh + nb)
+
+        def z_unit(s, rt):
+            for th in range(2):
+                z_bank(s, rt, th)
+            z_group(s, rt)
+
+        e_quarter(0)
+        nc.vector.tensor_copy(out=gain_sq[0:16, :], in_=gain_rows[:])
+        gain_bank = ps.tile([P, 4, P], F32, name="xt_ps", bufs=2)
+        nc.tensor.transpose(gain_bank[:, 0, :], gain_sq[:], ident[:])
+        comp_piece(0, 0)
+        nc.vector.tensor_copy(out=gain_col[:], in_=gain_bank[:, 0, 0:16])
+        x_transpose(0)
+        e_quarter(1)
+        comp_piece(1, 0)
+        x_transpose(1)
+        comp_piece(2, 0)
+        x_quant(0)
+        e_quarter(2)
+        comp_piece(3, 0)
+        x_transpose(2)
+        x_transpose(3)
+        z_unit(0, 0)
+        load_x(6)
+        load_x(7)
+        load_base(2)
+        load_base(3)
+        comp_piece(0, 1)
+        e_quarter(3)
+        x_transpose(4)
+        x_quant(1)
+        comp_piece(1, 1)
+        z_unit(1, 0)
+        x_transpose(5)
+        comp_piece(2, 1)
+        e_quant(*order[0])
+        e_quant(*order[1])
+        comp_piece(3, 1)
+        z_unit(0, 1)
+        e_quant(*order[2])
+        e_quant(*order[3])
+        z_quant(0, 0)
+        x_quant(2)
+        z_unit(1, 1)
+        z_quant(1, 0)
+        z_quant(0, 1)
+
+        def y_unit(i, jh):
+            y_matmul(i, jh)
+            y_mult(i, jh)
+
+        banks = [(2, 0, 0), (2, 0, 1), (2, 1, 0), (2, 1, 1), (3, 0, 0), (3, 0, 1), (3, 1, 0), (3, 1, 1)]
+        units = []
+        for s in range(PAIRS):
+            a, b = 2 * s, 2 * s + 1
+            if s in TR_PAIRS:
+                units += [("d", a, 0), ("t", s, 0), ("d", b, 0), ("b", a, 0), ("b", a, 1), ("b", b, 0), ("b", b, 1)]
+            else:
+                units += [("d", a, 0), ("d", a, 1), ("d", b, 0), ("d", b, 1)]
+        quants = {1: (1, 1), 3: (2, 0), 5: (2, 1), 7: (3, 0), 9: (3, 1)}
+        pending = []
+        for n, (kind, i, jh) in enumerate(units):
+            if kind == "d":
+                y_unit(i, jh)
+            elif kind == "t":
+                yt_matmul(i)
+            else:
+                yt_back(i, jh)
+            for p in pending:
+                y_add(*p)
+            pending = [(i, jh)] if kind == "d" else []
+            if n < 2:
+                x_transpose(6 + n)
+            if n == 2:
+                x_quant(3)
+            if n < len(banks):
+                z_bank(*banks[n])
+                if banks[n][2] == 1:
+                    z_group(*banks[n][:2])
+            if n in quants:
+                z_quant(*quants[n])
+            if n in (3, 5, 7, 8):
+                load_base(4 + (3, 5, 7, 8).index(n))

@@ -25,6 +25,7 @@ SLICE_ENGINE = ("vvvs", "vvvs", "vvvs", "vvvs")
 TR_PAIRS = (2, 3)
 G_ADD = {(i, jh) for i in range(8) for jh in range(2) if (jh == 0 and i < 7) or i in (1, 3)}
 MANUAL = True
+Z_GROUP_V = ((0, 1), (1, 1))
 
 
 def tile_mora_repeated_update_s12_kernel(tc, x, comp, gain, a_words, a_scales, d_words, d_scales, copy_gain, base, out):
@@ -57,15 +58,20 @@ def tile_mora_repeated_update_s12_kernel(tc, x, comp, gain, a_words, a_scales, d
         nc.vector.memset(ds_raw[:].rearrange("p g n -> p (g n)").bitcast(I32), 0)
         nc.vector.memset(warm[:], 0.0)
         nc.vector.memset(gain_sq[:], 0.0)
-        make_identity(nc, ident[:])
 
+        for q in range(4):
+            nc.gpsimd.dma_start(
+                out=ds_raw[32 * q : 32 * q + 4, :, :].bitcast(I32),
+                in_=d_scales[:, 4 * q : 4 * q + 4, :].rearrange("g r n -> r g n").bitcast(I32),
+            )
+        make_identity(nc, ident[:])
         for t in range(RT):
-            nc.scalar.dma_start(
+            nc.gpsimd.dma_start(
                 out=gain_rows[4 * t : 4 * t + 4, :].rearrange("t (q e) -> t q e", e=8),
                 in_=gain[512 * t : 512 * (t + 1)].rearrange("(q t e) -> t q e", t=4, e=8),
             )
         for c in range(C):
-            nc.scalar.dma_start(
+            nc.gpsimd.dma_start(
                 out=gain_rows[8 + 4 * c : 12 + 4 * c, :],
                 in_=copy_gain[c, 512:1024].rearrange("(b p) -> b p", p=P),
             )
@@ -81,7 +87,7 @@ def tile_mora_repeated_update_s12_kernel(tc, x, comp, gain, a_words, a_scales, d
             x_tiles[i] = xt
 
         def load_comp(g, rt):
-            ct = sb.tile([P, 4, 512], BF16, name="comp_raw", bufs=5, align_bytes=64)
+            ct = sb.tile([P, 4, 512], BF16, name="comp_raw", tag="half_block", bufs=8, align_bytes=64)
             nc.sync.dma_start(
                 out=ct[:],
                 in_=comp[512 * g : 512 * (g + 1), 512 * rt : 512 * (rt + 1)].rearrange("(p j) r -> p j r", j=4),
@@ -94,14 +100,13 @@ def tile_mora_repeated_update_s12_kernel(tc, x, comp, gain, a_words, a_scales, d
             base_tiles[i] = bt
 
         nc.sync.dma_start(out=a_raw[:].bitcast(I32), in_=a_words.rearrange("g p n -> p g n").bitcast(I32))
-        for raw, src in ((as_raw, a_scales), (ds_raw, d_scales)):
-            for q in range(4):
-                nc.sync.dma_start(
-                    out=raw[32 * q : 32 * q + 4, :, :].bitcast(I32),
-                    in_=src[:, 4 * q : 4 * q + 4, :].rearrange("g r n -> r g n").bitcast(I32),
-                )
-        nc.sync.dma_start(out=d_raw[:].bitcast(I32), in_=d_words.rearrange("g p n -> p g n").bitcast(I32))
+        for q in range(4):
+            nc.sync.dma_start(
+                out=as_raw[32 * q : 32 * q + 4, :, :].bitcast(I32),
+                in_=a_scales[:, 4 * q : 4 * q + 4, :].rearrange("g r n -> r g n").bitcast(I32),
+            )
         load_comp(0, 0)
+        nc.sync.dma_start(out=d_raw[:].bitcast(I32), in_=d_words.rearrange("g p n -> p g n").bitcast(I32))
         load_x(0)
         load_comp(1, 0)
         load_x(1)
@@ -227,10 +232,13 @@ def tile_mora_repeated_update_s12_kernel(tc, x, comp, gain, a_words, a_scales, d
 
         def z_group(s, rt):
             zg = sb.tile([P, 256, 4], BF16, name="zg", bufs=4, align_bytes=64)
-            nc.scalar.copy(out=zg[:], in_=zc_tiles[(s, rt)][:].rearrange("p t r -> p r t"))
             zg_tiles[(s, rt)] = zg
+            if (s, rt) not in Z_GROUP_V:
+                nc.scalar.copy(out=zg[:], in_=zc_tiles[(s, rt)][:].rearrange("p t r -> p r t"))
 
         def z_quant(s, rt):
+            if (s, rt) in Z_GROUP_V:
+                nc.vector.tensor_copy(out=zg_tiles[(s, rt)][:], in_=zc_tiles[(s, rt)][:].rearrange("p t r -> p r t"))
             codes = sb.tile([P, 256], U32, name="z_codes", bufs=8, align_bytes=64)
             scales = sb.tile([P, 256], U8, name="z_scales", bufs=8, align_bytes=64)
             nc.vector.quantize_mx(out=codes[:].bitcast(FP8), scales=scales[:], in_=zg_tiles[(s, rt)][:].rearrange("p r t -> p (r t)"))
@@ -264,7 +272,7 @@ def tile_mora_repeated_update_s12_kernel(tc, x, comp, gain, a_words, a_scales, d
         def y_mult(i, jh):
             cols = col_range(jh)
             width = cols.stop - cols.start
-            out_tiles[(i, jh)] = sb.tile([P, C, width], F32, name="out_sb", tag=f"out_sb{jh}", bufs=4 - 2 * jh, align_bytes=64)
+            out_tiles[(i, jh)] = sb.tile([P, C, width], F32, name="out_sb", tag="half_block", bufs=8, align_bytes=64)
             nc.vector.tensor_tensor(
                 out=out_tiles[(i, jh)][:],
                 in0=y_banks[(i, jh)][:].unsqueeze(1).to_broadcast([P, C, width]),
@@ -276,7 +284,11 @@ def tile_mora_repeated_update_s12_kernel(tc, x, comp, gain, a_words, a_scales, d
             cols = col_range(jh)
             eng = nc.gpsimd if (i, jh) in G_ADD else nc.vector
             ot = out_tiles[(i, jh)]
-            eng.tensor_tensor(out=ot[:], in0=ot[:], in1=base_tiles[i][:, :, cols], op=ADD)
+            if eng is nc.gpsimd:
+                for c in range(C):
+                    eng.tensor_tensor(out=ot[:, c, :], in0=ot[:, c, :], in1=base_tiles[i][:, c, cols], op=ADD)
+            else:
+                eng.tensor_tensor(out=ot[:], in0=ot[:], in1=base_tiles[i][:, :, cols], op=ADD)
             store(i, cols, ot)
 
         yt_tiles = {}
@@ -329,9 +341,11 @@ def tile_mora_repeated_update_s12_kernel(tc, x, comp, gain, a_words, a_scales, d
             a_permute(a_perm, a_raw, g, 4)
             a_permute(as_perm, as_raw, g, 2)
 
-        def comp_piece(g, rt):
-            comp_group(g, rt, 0, 4, "v")
-            comp_quant(g, rt)
+        def comp_step(n):
+            if n < 8:
+                comp_group(n % 4, n // 4, 0, 4, "v")
+            if n > 0:
+                comp_quant((n - 1) % 4, (n - 1) // 4)
 
         def e_quarter(n):
             rt, jh = order[n]
@@ -344,51 +358,50 @@ def tile_mora_repeated_update_s12_kernel(tc, x, comp, gain, a_words, a_scales, d
             z_group(s, rt)
 
         e_quarter(0)
-        nc.vector.tensor_copy(out=gain_sq[0:16, :], in_=gain_rows[:])
-        gain_bank = ps.tile([P, 4, P], F32, name="xt_ps", bufs=2)
-        nc.tensor.transpose(gain_bank[:, 0, :], gain_sq[:], ident[:])
-        comp_piece(0, 0)
-        nc.vector.tensor_copy(out=gain_col[:], in_=gain_bank[:, 0, 0:16])
+        comp_step(0)
         x_transpose(0)
+        comp_step(1)
+        nc.vector.tensor_copy(out=gain_sq[0:16, :], in_=gain_rows[:])
         e_quarter(1)
-        comp_piece(1, 0)
+        comp_step(2)
+        gain_bank = ps.tile([P, 4, P], F32, name="y_ps", bufs=2)
+        nc.tensor.transpose(gain_bank[:, 0, :], gain_sq[:], ident[:])
+        nc.vector.tensor_copy(out=gain_col[:], in_=gain_bank[:, 0, 0:16])
         x_transpose(1)
-        comp_piece(2, 0)
-        x_quant(0)
+        comp_step(3)
         e_quarter(2)
-        comp_piece(3, 0)
+        x_quant(0)
+        comp_step(4)
         x_transpose(2)
         x_transpose(3)
+        comp_step(5)
         z_unit(0, 0)
+        comp_step(6)
+        e_quarter(3)
+        e_quant(*order[0])
+        comp_step(7)
         load_x(6)
         load_x(7)
         load_base(2)
         load_base(3)
-        comp_piece(0, 1)
-        e_quarter(3)
         x_transpose(4)
-        x_quant(1)
-        comp_piece(1, 1)
-        z_unit(1, 0)
-        x_transpose(5)
-        comp_piece(2, 1)
-        e_quant(*order[0])
         e_quant(*order[1])
-        comp_piece(3, 1)
+        comp_step(8)
+        x_transpose(5)
+        x_quant(1)
         z_unit(0, 1)
         e_quant(*order[2])
-        e_quant(*order[3])
         z_quant(0, 0)
-        x_quant(2)
-        z_unit(1, 1)
-        z_quant(1, 0)
+        e_quant(*order[3])
+        z_unit(1, 0)
         z_quant(0, 1)
+        x_quant(2)
 
         def y_unit(i, jh):
             y_matmul(i, jh)
             y_mult(i, jh)
 
-        banks = [(2, 0, 0), (2, 0, 1), (2, 1, 0), (2, 1, 1), (3, 0, 0), (3, 0, 1), (3, 1, 0), (3, 1, 1)]
+        banks = [(1, 1, 0), (1, 1, 1), (2, 0, 0), (2, 0, 1), (2, 1, 0), (2, 1, 1), (3, 0, 0), (3, 0, 1), (3, 1, 0), (3, 1, 1)]
         units = []
         for s in range(PAIRS):
             a, b = 2 * s, 2 * s + 1
@@ -396,7 +409,7 @@ def tile_mora_repeated_update_s12_kernel(tc, x, comp, gain, a_words, a_scales, d
                 units += [("d", a, 0), ("t", s, 0), ("d", b, 0), ("b", a, 0), ("b", a, 1), ("b", b, 0), ("b", b, 1)]
             else:
                 units += [("d", a, 0), ("d", a, 1), ("d", b, 0), ("d", b, 1)]
-        quants = {1: (1, 1), 3: (2, 0), 5: (2, 1), 7: (3, 0), 9: (3, 1)}
+        quants = {0: (1, 0), 1: (1, 1), 4: (2, 0), 6: (2, 1), 8: (3, 0), 10: (3, 1)}
         pending = []
         for n, (kind, i, jh) in enumerate(units):
             if kind == "d":
@@ -408,9 +421,9 @@ def tile_mora_repeated_update_s12_kernel(tc, x, comp, gain, a_words, a_scales, d
             for p in pending:
                 y_add(*p)
             pending = [(i, jh)] if kind == "d" else []
-            if n < 2:
-                x_transpose(6 + n)
-            if n == 2:
+            if n in (2, 3):
+                x_transpose(4 + n)
+            if n == 4:
                 x_quant(3)
             if n < len(banks):
                 z_bank(*banks[n])

@@ -22,8 +22,8 @@ KG = K // 512
 RT = R // 512
 PAIRS = L // 256
 SLICE_ENGINE = ("vvvs", "vvvs", "vvvs", "vvvs")
-TR_PAIRS = (2, 3)
-G_ADD = {(i, jh) for i in range(8) for jh in range(2) if (jh == 0 and i < 7) or i in (1, 3)}
+TR = {(2, 1), (3, 0), (3, 1)}
+G_ADD = {(0, 0), (1, 0), (2, 0), (3, 0), (4, 0), (5, 0), (1, 1), (3, 1)}
 MANUAL = True
 Z_GROUP_V = ((0, 1), (1, 1))
 
@@ -49,9 +49,9 @@ def tile_mora_repeated_update_s12_kernel(tc, x, comp, gain, a_words, a_scales, d
         e_scales = one.tile([P, RT, N], U8, name="e_scales", align_bytes=64)
         cg = one.tile([P, C, N], BF16, name="cg", align_bytes=64)
         ident = one.tile([P, P], F32, name="ident", align_bytes=64)
-        gain_rows = one.tile([16, P], BF16, name="gain_rows", align_bytes=64)
+        gain_rows = one.tile([24, P], BF16, name="gain_rows", align_bytes=64)
         gain_sq = one.tile([P, P], F32, name="gain_sq", align_bytes=64)
-        gain_col = one.tile([P, 16], F32, name="gain_col", align_bytes=64)
+        gain_col = one.tile([P, 24], F32, name="gain_col", align_bytes=64)
         warm = one.tile([P, 1], F32, name="warm", align_bytes=64)
 
         nc.vector.memset(as_raw[:].rearrange("p g n -> p (g n)").bitcast(I32), 0)
@@ -59,22 +59,7 @@ def tile_mora_repeated_update_s12_kernel(tc, x, comp, gain, a_words, a_scales, d
         nc.vector.memset(warm[:], 0.0)
         nc.vector.memset(gain_sq[:], 0.0)
 
-        for q in range(4):
-            nc.gpsimd.dma_start(
-                out=ds_raw[32 * q : 32 * q + 4, :, :].bitcast(I32),
-                in_=d_scales[:, 4 * q : 4 * q + 4, :].rearrange("g r n -> r g n").bitcast(I32),
-            )
         make_identity(nc, ident[:])
-        for t in range(RT):
-            nc.gpsimd.dma_start(
-                out=gain_rows[4 * t : 4 * t + 4, :].rearrange("t (q e) -> t q e", e=8),
-                in_=gain[512 * t : 512 * (t + 1)].rearrange("(q t e) -> t q e", t=4, e=8),
-            )
-        for c in range(C):
-            nc.gpsimd.dma_start(
-                out=gain_rows[8 + 4 * c : 12 + 4 * c, :],
-                in_=copy_gain[c, 512:1024].rearrange("(b p) -> b p", p=P),
-            )
         nc.scalar.activation(out=warm[:], in_=warm[:], func=COPY)
 
         x_tiles = {}
@@ -99,18 +84,32 @@ def tile_mora_repeated_update_s12_kernel(tc, x, comp, gain, a_words, a_scales, d
             nc.sync.dma_start(out=bt[:].rearrange("p c n -> p (c n)"), in_=base[P * i : P * (i + 1), :])
             base_tiles[i] = bt
 
-        nc.sync.dma_start(out=a_raw[:].bitcast(I32), in_=a_words.rearrange("g p n -> p g n").bitcast(I32))
-        for q in range(4):
-            nc.sync.dma_start(
-                out=as_raw[32 * q : 32 * q + 4, :, :].bitcast(I32),
-                in_=a_scales[:, 4 * q : 4 * q + 4, :].rearrange("g r n -> r g n").bitcast(I32),
-            )
+        def load_scales(raw, src):
+            for q in range(4):
+                nc.sync.dma_start(
+                    out=raw[32 * q : 32 * q + 4, :, :].bitcast(I32),
+                    in_=src[:, 4 * q : 4 * q + 4, :].rearrange("g r n -> r g n").bitcast(I32),
+                )
+
         load_comp(0, 0)
-        nc.sync.dma_start(out=d_raw[:].bitcast(I32), in_=d_words.rearrange("g p n -> p g n").bitcast(I32))
         load_x(0)
+        nc.sync.dma_start(out=a_raw[:].bitcast(I32), in_=a_words.rearrange("g p n -> p g n").bitcast(I32))
+        nc.sync.dma_start(out=d_raw[:].bitcast(I32), in_=d_words.rearrange("g p n -> p g n").bitcast(I32))
+        load_scales(as_raw, a_scales)
+        load_scales(ds_raw, d_scales)
         load_comp(1, 0)
         load_x(1)
         load_comp(2, 0)
+        for t in range(RT):
+            nc.sync.dma_start(
+                out=gain_rows[4 * t : 4 * t + 4, :].rearrange("t (q e) -> t q e", e=8),
+                in_=gain[512 * t : 512 * (t + 1)].rearrange("(q t e) -> t q e", t=4, e=8),
+            )
+        for c in range(C):
+            nc.sync.dma_start(
+                out=gain_rows[8 + 8 * c : 16 + 8 * c, :],
+                in_=copy_gain[c, :].rearrange("(b p) -> b p", p=P),
+            )
         load_comp(3, 0)
         load_x(2)
         load_x(3)
@@ -293,13 +292,13 @@ def tile_mora_repeated_update_s12_kernel(tc, x, comp, gain, a_words, a_scales, d
 
         yt_tiles = {}
 
-        def yt_matmul(s):
-            yt = sb.tile([P, C, 4, 256], F32, name="yt", bufs=1, align_bytes=64)
+        def yt_matmul(s, jh):
+            yt = sb.tile([P, C, 4, 256], F32, name="yt", bufs=2, align_bytes=64)
             yt_banks = []
             for bb in range(2):
                 bank = ps.tile([P, 2, 256], F32, name="acc_ps", bufs=4)
                 for b2 in range(2):
-                    cols = slice(512 + P * (2 * bb + b2), 512 + P * (2 * bb + b2 + 1))
+                    cols = slice(512 * jh + P * (2 * bb + b2), 512 * jh + P * (2 * bb + b2 + 1))
                     for rt in range(RT):
                         codes, scales = z_codes[(s, rt)]
                         nc.tensor.matmul_mx(
@@ -314,18 +313,18 @@ def tile_mora_repeated_update_s12_kernel(tc, x, comp, gain, a_words, a_scales, d
                 yt_banks.append(bank)
             for c in range(C):
                 for b in range(4):
-                    k = 8 + 4 * c + b
+                    k = 8 + 8 * c + 4 * jh + b
                     nc.scalar.activation(out=yt[:, c, b, :], in_=yt_banks[b // 2][:, b % 2, :], func=COPY, scale=gain_col[:, k : k + 1])
-            yt_tiles[s] = yt
+            yt_tiles[(s, jh)] = yt
 
-        def yt_back(i, c):
+        def yt_back(i, jh, c):
             s, h = divmod(i, 2)
             bank = ps.tile([P, 4, P], F32, name="xt_ps", bufs=2)
             for b in range(4):
-                nc.tensor.transpose(bank[:, b, :], yt_tiles[s][:, c, b, P * h : P * (h + 1)], ident[:])
-            ot = sb.tile([P, 512], F32, name="out_sb", tag="out_tr", bufs=6, align_bytes=64)
-            nc.vector.tensor_tensor(out=ot[:], in0=bank[:].rearrange("p b t -> p (b t)"), in1=base_tiles[i][:, c, 512:1024], op=ADD)
-            nc.sync.dma_start(out=out[P * i : P * (i + 1), N * c + 512 : N * (c + 1)], in_=ot[:])
+                nc.tensor.transpose(bank[:, b, :], yt_tiles[(s, jh)][:, c, b, P * h : P * (h + 1)], ident[:])
+            ot = sb.tile([P, 512], F32, name="out_sb", tag="out_tr", bufs=8, align_bytes=64)
+            nc.vector.tensor_tensor(out=ot[:], in0=bank[:].rearrange("p b t -> p (b t)"), in1=base_tiles[i][:, c, 512 * jh : 512 * (jh + 1)], op=ADD)
+            nc.sync.dma_start(out=out[P * i : P * (i + 1), N * c + 512 * jh : N * c + 512 * (jh + 1)], in_=ot[:])
 
         def store(i, cols, ot):
             nc.sync.dma_start(out=out[P * i : P * (i + 1), :].rearrange("p (c n) -> p c n", c=C)[:, :, cols], in_=ot[:])
@@ -337,9 +336,6 @@ def tile_mora_repeated_update_s12_kernel(tc, x, comp, gain, a_words, a_scales, d
             )
 
         order = [(rt, jh) for jh in range(2) for rt in range(2)]
-        for g in range(2):
-            a_permute(a_perm, a_raw, g, 4)
-            a_permute(as_perm, as_raw, g, 2)
 
         def comp_step(n):
             if n < 8:
@@ -357,16 +353,19 @@ def tile_mora_repeated_update_s12_kernel(tc, x, comp, gain, a_words, a_scales, d
                 z_bank(s, rt, th)
             z_group(s, rt)
 
-        e_quarter(0)
-        comp_step(0)
+        comp_group(0, 0, 0, 4, "v")
         x_transpose(0)
+        for g in range(2):
+            a_permute(a_perm, a_raw, g, 4)
+            a_permute(as_perm, as_raw, g, 2)
+        e_quarter(0)
         comp_step(1)
-        nc.vector.tensor_copy(out=gain_sq[0:16, :], in_=gain_rows[:])
         e_quarter(1)
         comp_step(2)
+        nc.vector.tensor_copy(out=gain_sq[0:24, :], in_=gain_rows[:])
         gain_bank = ps.tile([P, 4, P], F32, name="y_ps", bufs=2)
         nc.tensor.transpose(gain_bank[:, 0, :], gain_sq[:], ident[:])
-        nc.vector.tensor_copy(out=gain_col[:], in_=gain_bank[:, 0, 0:16])
+        nc.vector.tensor_copy(out=gain_col[:], in_=gain_bank[:, 0, 0:24])
         x_transpose(1)
         comp_step(3)
         e_quarter(2)
@@ -402,22 +401,20 @@ def tile_mora_repeated_update_s12_kernel(tc, x, comp, gain, a_words, a_scales, d
             y_mult(i, jh)
 
         banks = [(1, 1, 0), (1, 1, 1), (2, 0, 0), (2, 0, 1), (2, 1, 0), (2, 1, 1), (3, 0, 0), (3, 0, 1), (3, 1, 0), (3, 1, 1)]
-        units = []
-        for s in range(PAIRS):
-            a, b = 2 * s, 2 * s + 1
-            if s in TR_PAIRS:
-                units += [("d", a, 0), ("t", s, 0), ("d", b, 0), ("b", a, 0), ("b", a, 1), ("b", b, 0), ("b", b, 1)]
-            else:
-                units += [("d", a, 0), ("d", a, 1), ("d", b, 0), ("d", b, 1)]
-        quants = {0: (1, 0), 1: (1, 1), 4: (2, 0), 6: (2, 1), 8: (3, 0), 10: (3, 1)}
+        units = [("d", i, jh) for i in range(4) for jh in range(2)]
+        units += [("d", 4, 0), ("d", 5, 0), ("t", 2, 1), ("t", 3, 0)]
+        units += [("b", i, (1, c)) for i in (4, 5) for c in range(C)]
+        units += [("t", 3, 1)]
+        units += [("b", i, (jh, c)) for jh in range(2) for i in (6, 7) for c in range(C)]
+        quants = {0: (1, 0), 1: (1, 1), 4: (2, 0), 6: (2, 1), 8: (3, 0), 9: (3, 1)}
         pending = []
         for n, (kind, i, jh) in enumerate(units):
             if kind == "d":
                 y_unit(i, jh)
             elif kind == "t":
-                yt_matmul(i)
+                yt_matmul(i, jh)
             else:
-                yt_back(i, jh)
+                yt_back(i, *jh)
             for p in pending:
                 y_add(*p)
             pending = [(i, jh)] if kind == "d" else []

@@ -18,14 +18,11 @@ L, K, R, N, C = 1024, 2048, 1024, 1024, 2
 FLOPS = 2 * L * K * R + 2 * R * R * N + 2 * L * R * N
 
 P = 128
-KG = K // 512
-RT = R // 512
-PAIRS = L // 256
-SLICE_ENGINE = ("vvvs", "vvvs", "vvvs", "vvvs")
-TR = {(2, 1), (3, 0), (3, 1)}
-G_ADD = {(0, 0), (1, 0), (2, 0), (3, 0), (4, 0), (5, 0), (1, 1), (3, 1)}
-MANUAL = True
-Z_GROUP_V = ((0, 1), (1, 1))
+PASS = 512
+KG = K // PASS
+RT = R // PASS
+PAIR = 256
+HALF = 512
 
 
 def tile_mora_repeated_update_s12_kernel(tc, x, comp, gain, a_words, a_scales, d_words, d_scales, copy_gain, base, out):
@@ -34,15 +31,14 @@ def tile_mora_repeated_update_s12_kernel(tc, x, comp, gain, a_words, a_scales, d
         one = ctx.enter_context(tc.tile_pool(name="one", bufs=1))
         sb = ctx.enter_context(tc.tile_pool(name="sb", bufs=2))
         ps = ctx.enter_context(tc.psum_pool(name="ps", bufs=2))
-        if MANUAL:
-            ctx.enter_context(tc.manual_schedule())
+        ctx.enter_context(tc.manual_schedule())
 
-        a_raw = one.tile([P, 2, 2048], U8, name="a_raw", align_bytes=64)
-        a_perm = one.tile([P, 2, 2048], U8, name="a_perm", align_bytes=64)
-        d_raw = one.tile([P, 2, 2048], U8, name="d_raw", align_bytes=64)
-        as_raw = one.tile([P, 2, 1024], U8, name="as_raw", align_bytes=64)
-        as_perm = one.tile([P, 2, 1024], U8, name="as_perm", align_bytes=64)
-        ds_raw = one.tile([P, 2, 1024], U8, name="ds_raw", align_bytes=64)
+        a_raw = one.tile([P, 2, 2 * R], U8, name="a_raw", align_bytes=64)
+        a_perm = one.tile([P, 2, 2 * R], U8, name="a_perm", align_bytes=64)
+        a_scales_raw = one.tile([P, 2, R], U8, name="a_scales_raw", align_bytes=64)
+        a_scales_perm = one.tile([P, 2, R], U8, name="a_scales_perm", align_bytes=64)
+        d_sb = one.tile([P, 2, 2 * N], U8, name="d_sb", align_bytes=64)
+        d_scales_sb = one.tile([P, 2, N], U8, name="d_scales_sb", align_bytes=64)
         comp_codes = one.tile([P, KG, R], U32, name="comp_codes", align_bytes=64)
         comp_scales = one.tile([P, KG, R], U8, name="comp_scales", align_bytes=64)
         e_codes = one.tile([P, RT, N], U32, name="e_codes", align_bytes=64)
@@ -54,80 +50,80 @@ def tile_mora_repeated_update_s12_kernel(tc, x, comp, gain, a_words, a_scales, d
         gain_col = one.tile([P, 24], F32, name="gain_col", align_bytes=64)
         warm = one.tile([P, 1], F32, name="warm", align_bytes=64)
 
-        nc.vector.memset(as_raw[:].rearrange("p g n -> p (g n)").bitcast(I32), 0)
-        nc.vector.memset(ds_raw[:].rearrange("p g n -> p (g n)").bitcast(I32), 0)
+        nc.vector.memset(a_scales_raw[:].rearrange("p g n -> p (g n)").bitcast(I32), 0)
+        nc.vector.memset(d_scales_sb[:].rearrange("p g n -> p (g n)").bitcast(I32), 0)
         nc.vector.memset(warm[:], 0.0)
         nc.vector.memset(gain_sq[:], 0.0)
-
         make_identity(nc, ident[:])
         nc.scalar.activation(out=warm[:], in_=warm[:], func=COPY)
 
-        x_tiles = {}
-        comp_raw = {}
-        base_tiles = {}
+        x_tiles, comp_raw, base_tiles = {}, {}, {}
 
         def load_x(i):
-            xt = sb.tile([P, K], BF16, name="x_in", bufs=4, align_bytes=64)
-            nc.sync.dma_start(out=xt[:], in_=x[P * i : P * (i + 1), :])
-            x_tiles[i] = xt
+            x_tiles[i] = sb.tile([P, K], BF16, name="x_in", tag="token_rows", bufs=9, align_bytes=64)
+            nc.sync.dma_start(out=x_tiles[i][:], in_=x[P * i : P * (i + 1), :])
 
-        def load_comp(g, rt):
-            ct = sb.tile([P, 4, 512], BF16, name="comp_raw", tag="half_block", bufs=8, align_bytes=64)
-            nc.sync.dma_start(
-                out=ct[:],
-                in_=comp[512 * g : 512 * (g + 1), 512 * rt : 512 * (rt + 1)].rearrange("(p j) r -> p j r", j=4),
-            )
-            comp_raw[(g, rt)] = ct
+        def load_comp(n):
+            rt, g = divmod(n, KG)
+            comp_raw[n] = sb.tile([P, 4, PASS], BF16, name="comp_raw", tag="half_block", bufs=8, align_bytes=64)
+            block = comp[PASS * g : PASS * (g + 1), PASS * rt : PASS * (rt + 1)]
+            nc.sync.dma_start(out=comp_raw[n][:], in_=block.rearrange("(p j) r -> p j r", j=4))
 
         def load_base(i):
-            bt = sb.tile([P, C, N], BF16, name="base_in", bufs=4, align_bytes=64)
-            nc.sync.dma_start(out=bt[:].rearrange("p c n -> p (c n)"), in_=base[P * i : P * (i + 1), :])
-            base_tiles[i] = bt
+            base_tiles[i] = sb.tile([P, C, N], BF16, name="base_in", tag="token_rows", bufs=9, align_bytes=64)
+            nc.sync.dma_start(out=base_tiles[i][:].rearrange("p c n -> p (c n)"), in_=base[P * i : P * (i + 1), :])
 
-        def load_scales(raw, src):
+        def load_words(tile, src):
+            nc.sync.dma_start(out=tile[:].bitcast(I32), in_=src.rearrange("g p n -> p g n").bitcast(I32))
+
+        def load_scales(tile, src):
             for q in range(4):
                 nc.sync.dma_start(
-                    out=raw[32 * q : 32 * q + 4, :, :].bitcast(I32),
+                    out=tile[32 * q : 32 * q + 4, :, :].bitcast(I32),
                     in_=src[:, 4 * q : 4 * q + 4, :].rearrange("g r n -> r g n").bitcast(I32),
                 )
 
-        load_comp(0, 0)
-        load_x(0)
-        nc.sync.dma_start(out=a_raw[:].bitcast(I32), in_=a_words.rearrange("g p n -> p g n").bitcast(I32))
-        nc.sync.dma_start(out=d_raw[:].bitcast(I32), in_=d_words.rearrange("g p n -> p g n").bitcast(I32))
-        load_scales(as_raw, a_scales)
-        load_scales(ds_raw, d_scales)
-        load_comp(1, 0)
-        load_x(1)
-        load_comp(2, 0)
-        for t in range(RT):
-            nc.sync.dma_start(
-                out=gain_rows[4 * t : 4 * t + 4, :].rearrange("t (q e) -> t q e", e=8),
-                in_=gain[512 * t : 512 * (t + 1)].rearrange("(q t e) -> t q e", t=4, e=8),
-            )
-        for c in range(C):
-            nc.sync.dma_start(
-                out=gain_rows[8 + 8 * c : 16 + 8 * c, :],
-                in_=copy_gain[c, :].rearrange("(b p) -> b p", p=P),
-            )
-        load_comp(3, 0)
-        load_x(2)
-        load_x(3)
-        for g in range(KG):
-            load_comp(g, 1)
-        load_x(4)
-        load_x(5)
-        nc.sync.dma_start(out=cg[:].rearrange("p c n -> p (c n)"), in_=copy_gain.rearrange("c n -> (c n)").partition_broadcast(P))
-        load_base(0)
-        load_base(1)
+        def load_gains():
+            for rt in range(RT):
+                nc.sync.dma_start(
+                    out=gain_rows[4 * rt : 4 * rt + 4, :].rearrange("t (q e) -> t q e", e=8),
+                    in_=gain[PASS * rt : PASS * (rt + 1)].rearrange("(q t e) -> t q e", t=4, e=8),
+                )
+            for c in range(C):
+                nc.sync.dma_start(
+                    out=gain_rows[8 + 8 * c : 16 + 8 * c, :],
+                    in_=copy_gain[c, :].rearrange("(b p) -> b p", p=P),
+                )
 
-        xg_tiles = {}
-        x_codes = {}
+        load_comp(0)
+        load_x(0)
+        load_words(a_raw, a_words)
+        load_words(d_sb, d_words)
+        load_scales(a_scales_raw, a_scales)
+        load_scales(d_scales_sb, d_scales)
+        load_comp(1)
+        load_x(1)
+        load_comp(2)
+        load_x(2)
+        load_gains()
+        load_x(3)
+        for n in range(3, 7):
+            load_comp(n)
+        load_x(4)
+        load_comp(7)
+        load_x(5)
+        load_x(6)
+        load_x(7)
+        nc.sync.dma_start(out=cg[:].rearrange("p c n -> p (c n)"), in_=copy_gain.rearrange("c n -> (c n)").partition_broadcast(P))
+        for i in range(8):
+            load_base(i)
+
+        xg, x_codes = {}, {}
 
         def x_transpose(i):
             s, h = divmod(i, 2)
             if h == 0:
-                xg_tiles[s] = sb.tile([P, KG, 256, 2], F32, name="xg", align_bytes=64)
+                xg[s] = sb.tile([P, KG, PAIR, 2], F32, name="xg", align_bytes=64)
             words = x_tiles[i][:].bitcast(F32)
             for b in range(2):
                 bank = ps.tile([P, 4, P], F32, name="xt_ps", bufs=2)
@@ -136,125 +132,124 @@ def tile_mora_repeated_update_s12_kernel(tc, x, comp, gain, a_words, a_scales, d
                         w0 = 256 * (2 * b + g2) + u
                         nc.tensor.transpose(bank[:, 2 * g2 + u, :], words[:, w0 : w0 + 255 : 2], ident[:])
                 nc.scalar.copy(
-                    out=xg_tiles[s][:, 2 * b : 2 * b + 2, P * h : P * (h + 1), :],
+                    out=xg[s][:, 2 * b : 2 * b + 2, P * h : P * (h + 1), :],
                     in_=bank[:].rearrange("p (g u) r -> p g r u", u=2),
                 )
 
         def x_quant(s):
-            codes = sb.tile([P, KG, 256], U32, name="x_codes", bufs=3, align_bytes=64)
-            scales = sb.tile([P, KG, 256], U8, name="x_scales", bufs=3, align_bytes=64)
+            codes = sb.tile([P, KG, PAIR], U32, name="x_codes", bufs=3, align_bytes=64)
+            scales = sb.tile([P, KG, PAIR], U8, name="x_scales", bufs=3, align_bytes=64)
             nc.vector.quantize_mx(
                 out=codes[:].rearrange("p g r -> p (g r)").bitcast(FP8),
                 scales=scales[:].rearrange("p g r -> p (g r)"),
-                in_=xg_tiles[s][:].rearrange("p g r u -> p (g r u)").bitcast(BF16),
+                in_=xg[s][:].rearrange("p g r u -> p (g r u)").bitcast(BF16),
             )
             x_codes[s] = (codes, scales)
 
         comp_grouped = {}
 
-        def comp_group(g, rt, t0, t1, eng):
-            key = (g, rt)
-            if key not in comp_grouped:
-                comp_grouped[key] = sb.tile([P, 4, 16, 8, 4], BF16, name="comp_grouped", bufs=3, align_bytes=64)
-            dst = comp_grouped[key][:, t0:t1, :, :, :]
-            src = comp_raw[key][:].rearrange("p j (q t e) -> p t q e j", t=4, e=8)[:, t0:t1, :, :, :]
-            if t1 - t0 == 1:
-                dst = dst.rearrange("p t q e j -> p (t q) e j")
-                src = comp_raw[key][:].rearrange("p j (q t e) -> p t q e j", t=4, e=8)[:, t0, :, :, :]
-            if eng == "v":
-                nc.vector.tensor_copy(out=dst, in_=src)
-            else:
-                nc.scalar.copy(out=dst, in_=src)
+        def comp_group(n):
+            comp_grouped[n] = sb.tile([P, 4, 16, 8, 4], BF16, name="comp_grouped", bufs=3, align_bytes=64)
+            nc.vector.tensor_copy(
+                out=comp_grouped[n][:],
+                in_=comp_raw[n][:].rearrange("p j (q t e) -> p t q e j", t=4, e=8),
+            )
 
-        def comp_quant(g, rt):
-            cols = slice(512 * rt, 512 * (rt + 1))
+        def comp_quant(n):
+            rt, g = divmod(n, KG)
+            cols = slice(PASS * rt, PASS * (rt + 1))
             nc.vector.quantize_mx(
                 out=comp_codes[:, g, cols].bitcast(FP8),
                 scales=comp_scales[:, g, cols],
-                in_=comp_grouped[(g, rt)][:].rearrange("p t q e j -> p (t q e j)"),
+                in_=comp_grouped[n][:].rearrange("p t q e j -> p (t q e j)"),
             )
 
-        eg_tiles = {}
+        def gains_to_columns():
+            nc.vector.tensor_copy(out=gain_sq[0:24, :], in_=gain_rows[:])
+            bank = ps.tile([P, 4, P], F32, name="y_ps", bufs=2)
+            nc.tensor.transpose(bank[:, 0, :], gain_sq[:], ident[:])
+            nc.vector.tensor_copy(out=gain_col[:], in_=bank[:, 0, 0:24])
 
-        def e_block(rt, nb):
-            bank = ps.tile([P, 4, P], F32, name="acc_ps", bufs=4)
-            for t in range(4):
-                col = 512 * rt + 128 * t
-                for g in range(2):
-                    nc.tensor.matmul_mx(
-                        out=bank[:, t, :],
-                        lhsT=a_perm[:, g, 2 * col : 2 * col + 256].bitcast(FP4),
-                        lhsT_scale=as_perm[:, g, col : col + 128],
-                        rhs=d_raw[:, g, 256 * nb : 256 * (nb + 1)].bitcast(FP4),
-                        rhs_scale=ds_raw[:, g, 128 * nb : 128 * (nb + 1)],
-                        start=(g == 0),
-                        stop=(g == 1),
+        eg = {}
+
+        def permute_a():
+            for g in range(2):
+                for dst, src, w in ((a_perm, a_raw, 4), (a_scales_perm, a_scales_raw, 2)):
+                    nc.vector.tensor_copy(
+                        out=dst[:, g, :].bitcast(I32).rearrange("p (r t q w) -> p r t q w", r=RT, t=4, w=w),
+                        in_=src[:, g, :].bitcast(I32).rearrange("p (r q t w) -> p r t q w", r=RT, t=4, w=w),
                     )
-            key = (rt, nb // 4)
-            if nb % 4 == 0:
-                eg_tiles[key] = sb.tile([P, 512, 4], BF16, name="eg", bufs=4, align_bytes=64)
-            c0 = 128 * (nb % 4)
-            nc.scalar.copy(out=eg_tiles[key][:, c0 : c0 + 128, :], in_=bank[:].rearrange("p t n -> p n t"))
 
-        def e_quant(rt, jh):
+        def e_blocks(quarter, half):
+            jh, rt = divmod(quarter, RT)
+            if half == 0:
+                eg[quarter] = sb.tile([P, HALF, 4], BF16, name="eg", bufs=4, align_bytes=64)
+            for b in (2 * half, 2 * half + 1):
+                nb = 4 * jh + b
+                bank = ps.tile([P, 4, P], F32, name="acc_ps", bufs=4)
+                for t in range(4):
+                    col = PASS * rt + P * t
+                    for g in range(2):
+                        nc.tensor.matmul_mx(
+                            out=bank[:, t, :],
+                            lhsT=a_perm[:, g, 2 * col : 2 * (col + P)].bitcast(FP4),
+                            lhsT_scale=a_scales_perm[:, g, col : col + P],
+                            rhs=d_sb[:, g, 2 * P * nb : 2 * P * (nb + 1)].bitcast(FP4),
+                            rhs_scale=d_scales_sb[:, g, P * nb : P * (nb + 1)],
+                            start=(g == 0),
+                            stop=(g == 1),
+                        )
+                nc.scalar.copy(out=eg[quarter][:, P * b : P * (b + 1), :], in_=bank[:].rearrange("p t n -> p n t"))
+
+        def e_quant(quarter):
+            jh, rt = divmod(quarter, RT)
+            cols = slice(HALF * jh, HALF * (jh + 1))
             nc.vector.quantize_mx(
-                out=e_codes[:, rt, 512 * jh : 512 * (jh + 1)].bitcast(FP8),
-                scales=e_scales[:, rt, 512 * jh : 512 * (jh + 1)],
-                in_=eg_tiles[(rt, jh)][:].rearrange("p n t -> p (n t)"),
+                out=e_codes[:, rt, cols].bitcast(FP8),
+                scales=e_scales[:, rt, cols],
+                in_=eg[quarter][:].rearrange("p n t -> p (n t)"),
             )
 
-        zc_tiles = {}
-        zg_tiles = {}
-        z_codes = {}
+        zc, zg, z_codes = {}, {}, {}
 
-        def z_bank(s, rt, th):
+        def z_matmul(s, rt):
             codes, scales = x_codes[s]
-            if th == 0:
-                zc_tiles[(s, rt)] = sb.tile([P, 4, 256], BF16, name="zc", bufs=3, align_bytes=64)
-            zc = zc_tiles[(s, rt)]
-            bank = ps.tile([P, 2, 256], F32, name="acc_ps", bufs=4)
-            for h in range(2):
-                col = 512 * rt + 128 * (2 * th + h)
-                for g in range(KG):
-                    nc.tensor.matmul_mx(
-                        out=bank[:, h, :],
-                        lhsT=comp_codes[:, g, col : col + 128].bitcast(FP8),
-                        lhsT_scale=comp_scales[:, g, col : col + 128],
-                        rhs=codes[:, g, :].bitcast(FP8),
-                        rhs_scale=scales[:, g, :],
-                        start=(g == 0),
-                        stop=(g == KG - 1),
-                    )
-            for h in range(2):
-                t = 2 * th + h
-                nc.scalar.activation(out=zc[:, t, :], in_=bank[:, h, :], func=COPY, scale=gain_col[:, 4 * rt + t : 4 * rt + t + 1])
+            zc[(s, rt)] = sb.tile([P, 4, PAIR], BF16, name="zc", bufs=3, align_bytes=64)
+            for th in range(2):
+                bank = ps.tile([P, 2, PAIR], F32, name="acc_ps", bufs=4)
+                for h in range(2):
+                    col = PASS * rt + P * (2 * th + h)
+                    for g in range(KG):
+                        nc.tensor.matmul_mx(
+                            out=bank[:, h, :],
+                            lhsT=comp_codes[:, g, col : col + P].bitcast(FP8),
+                            lhsT_scale=comp_scales[:, g, col : col + P],
+                            rhs=codes[:, g, :].bitcast(FP8),
+                            rhs_scale=scales[:, g, :],
+                            start=(g == 0),
+                            stop=(g == KG - 1),
+                        )
+                for h in range(2):
+                    t = 2 * th + h
+                    k = 4 * rt + t
+                    nc.scalar.activation(out=zc[(s, rt)][:, t, :], in_=bank[:, h, :], func=COPY, scale=gain_col[:, k : k + 1])
 
-        def z_group(s, rt):
-            zg = sb.tile([P, 256, 4], BF16, name="zg", bufs=4, align_bytes=64)
-            zg_tiles[(s, rt)] = zg
-            if (s, rt) not in Z_GROUP_V:
-                nc.scalar.copy(out=zg[:], in_=zc_tiles[(s, rt)][:].rearrange("p t r -> p r t"))
+        def z_group(s, rt, copy):
+            zg[(s, rt)] = sb.tile([P, PAIR, 4], BF16, name="zg", bufs=4, align_bytes=64)
+            copy(out=zg[(s, rt)][:], in_=zc[(s, rt)][:].rearrange("p t r -> p r t"))
 
         def z_quant(s, rt):
-            if (s, rt) in Z_GROUP_V:
-                nc.vector.tensor_copy(out=zg_tiles[(s, rt)][:], in_=zc_tiles[(s, rt)][:].rearrange("p t r -> p r t"))
-            codes = sb.tile([P, 256], U32, name="z_codes", bufs=8, align_bytes=64)
-            scales = sb.tile([P, 256], U8, name="z_scales", bufs=8, align_bytes=64)
-            nc.vector.quantize_mx(out=codes[:].bitcast(FP8), scales=scales[:], in_=zg_tiles[(s, rt)][:].rearrange("p r t -> p (r t)"))
+            codes = sb.tile([P, PAIR], U32, name="z_codes", bufs=8, align_bytes=64)
+            scales = sb.tile([P, PAIR], U8, name="z_scales", bufs=8, align_bytes=64)
+            nc.vector.quantize_mx(out=codes[:].bitcast(FP8), scales=scales[:], in_=zg[(s, rt)][:].rearrange("p r t -> p (r t)"))
             z_codes[(s, rt)] = (codes, scales)
 
-        y_banks = {}
-        out_tiles = {}
+        products, yt = {}, {}
 
-
-        def col_range(jh):
-            return slice(512 * jh, 512 * (jh + 1))
-
-        def y_matmul(i, jh):
+        def y_direct(i, jh):
             s, h = divmod(i, 2)
-            cols = col_range(jh)
-            width = cols.stop - cols.start
-            bank = ps.tile([P, width], F32, name="y_ps", tag="y_ps", bufs=2)
+            cols = slice(HALF * jh, HALF * (jh + 1))
+            bank = ps.tile([P, HALF], F32, name="y_ps", bufs=2)
             for rt in range(RT):
                 codes, scales = z_codes[(s, rt)]
                 nc.tensor.matmul_mx(
@@ -266,167 +261,152 @@ def tile_mora_repeated_update_s12_kernel(tc, x, comp, gain, a_words, a_scales, d
                     start=(rt == 0),
                     stop=(rt == RT - 1),
                 )
-            y_banks[(i, jh)] = bank
-
-        def y_mult(i, jh):
-            cols = col_range(jh)
-            width = cols.stop - cols.start
-            out_tiles[(i, jh)] = sb.tile([P, C, width], F32, name="out_sb", tag="half_block", bufs=8, align_bytes=64)
+            products[(i, jh)] = sb.tile([P, C, HALF], F32, name="product", tag="half_block", bufs=8, align_bytes=64)
             nc.vector.tensor_tensor(
-                out=out_tiles[(i, jh)][:],
-                in0=y_banks[(i, jh)][:].unsqueeze(1).to_broadcast([P, C, width]),
+                out=products[(i, jh)][:],
+                in0=bank[:].unsqueeze(1).to_broadcast([P, C, HALF]),
                 in1=cg[:, :, cols],
                 op=MULT,
             )
 
-        def y_add(i, jh):
-            cols = col_range(jh)
-            eng = nc.gpsimd if (i, jh) in G_ADD else nc.vector
-            ot = out_tiles[(i, jh)]
-            if eng is nc.gpsimd:
-                for c in range(C):
-                    eng.tensor_tensor(out=ot[:, c, :], in0=ot[:, c, :], in1=base_tiles[i][:, c, cols], op=ADD)
-            else:
-                eng.tensor_tensor(out=ot[:], in0=ot[:], in1=base_tiles[i][:, :, cols], op=ADD)
-            store(i, cols, ot)
+        def add_base(i, jh):
+            cols = slice(HALF * jh, HALF * (jh + 1))
+            product = products[(i, jh)]
+            nc.vector.tensor_tensor(out=product[:], in0=product[:], in1=base_tiles[i][:, :, cols], op=ADD)
+            nc.sync.dma_start(out=out[P * i : P * (i + 1), :].rearrange("p (c n) -> p c n", c=C)[:, :, cols], in_=product[:])
 
-        yt_tiles = {}
-
-        def yt_matmul(s, jh):
-            yt = sb.tile([P, C, 4, 256], F32, name="yt", bufs=2, align_bytes=64)
-            yt_banks = []
-            for bb in range(2):
-                bank = ps.tile([P, 2, 256], F32, name="acc_ps", bufs=4)
-                for b2 in range(2):
-                    cols = slice(512 * jh + P * (2 * bb + b2), 512 * jh + P * (2 * bb + b2 + 1))
-                    for rt in range(RT):
-                        codes, scales = z_codes[(s, rt)]
-                        nc.tensor.matmul_mx(
-                            out=bank[:, b2, :],
-                            lhsT=e_codes[:, rt, cols].bitcast(FP8),
-                            lhsT_scale=e_scales[:, rt, cols],
-                            rhs=codes[:].bitcast(FP8),
-                            rhs_scale=scales[:],
-                            start=(rt == 0),
-                            stop=(rt == RT - 1),
-                        )
-                yt_banks.append(bank)
+        def y_transposed(s, jh):
+            banks = []
+            for b in range(4):
+                if b % 2 == 0:
+                    banks.append(ps.tile([P, 2, PAIR], F32, name="acc_ps", bufs=4))
+                cols = slice(HALF * jh + P * b, HALF * jh + P * (b + 1))
+                for rt in range(RT):
+                    codes, scales = z_codes[(s, rt)]
+                    nc.tensor.matmul_mx(
+                        out=banks[b // 2][:, b % 2, :],
+                        lhsT=e_codes[:, rt, cols].bitcast(FP8),
+                        lhsT_scale=e_scales[:, rt, cols],
+                        rhs=codes[:].bitcast(FP8),
+                        rhs_scale=scales[:],
+                        start=(rt == 0),
+                        stop=(rt == RT - 1),
+                    )
+            yt[(s, jh)] = sb.tile([P, C, 4, PAIR], F32, name="yt", align_bytes=64)
             for c in range(C):
                 for b in range(4):
                     k = 8 + 8 * c + 4 * jh + b
-                    nc.scalar.activation(out=yt[:, c, b, :], in_=yt_banks[b // 2][:, b % 2, :], func=COPY, scale=gain_col[:, k : k + 1])
-            yt_tiles[(s, jh)] = yt
+                    nc.scalar.activation(out=yt[(s, jh)][:, c, b, :], in_=banks[b // 2][:, b % 2, :], func=COPY, scale=gain_col[:, k : k + 1])
 
-        def yt_back(i, jh, c):
+        def turn_back(i, jh, c):
             s, h = divmod(i, 2)
             bank = ps.tile([P, 4, P], F32, name="xt_ps", bufs=2)
             for b in range(4):
-                nc.tensor.transpose(bank[:, b, :], yt_tiles[(s, jh)][:, c, b, P * h : P * (h + 1)], ident[:])
-            ot = sb.tile([P, 512], F32, name="out_sb", tag="out_tr", bufs=8, align_bytes=64)
-            nc.vector.tensor_tensor(out=ot[:], in0=bank[:].rearrange("p b t -> p (b t)"), in1=base_tiles[i][:, c, 512 * jh : 512 * (jh + 1)], op=ADD)
-            nc.sync.dma_start(out=out[P * i : P * (i + 1), N * c + 512 * jh : N * c + 512 * (jh + 1)], in_=ot[:])
+                nc.tensor.transpose(bank[:, b, :], yt[(s, jh)][:, c, b, P * h : P * (h + 1)], ident[:])
+            quarter = sb.tile([P, HALF], F32, name="quarter", bufs=8, align_bytes=64)
+            cols = slice(HALF * jh, HALF * (jh + 1))
+            nc.vector.tensor_tensor(out=quarter[:], in0=bank[:].rearrange("p b t -> p (b t)"), in1=base_tiles[i][:, c, cols], op=ADD)
+            nc.sync.dma_start(out=out[P * i : P * (i + 1), N * c + HALF * jh : N * c + HALF * (jh + 1)], in_=quarter[:])
 
-        def store(i, cols, ot):
-            nc.sync.dma_start(out=out[P * i : P * (i + 1), :].rearrange("p (c n) -> p c n", c=C)[:, :, cols], in_=ot[:])
-
-        def a_permute(dst, raw, g, w):
-            nc.vector.tensor_copy(
-                out=dst[:, g, :].bitcast(I32).rearrange("p (r t q w) -> p r t q w", r=2, t=4, w=w),
-                in_=raw[:, g, :].bitcast(I32).rearrange("p (r q t w) -> p r t q w", r=2, t=4, w=w),
-            )
-
-        order = [(rt, jh) for jh in range(2) for rt in range(2)]
-
-        def comp_step(n):
-            if n < 8:
-                comp_group(n % 4, n // 4, 0, 4, "v")
-            if n > 0:
-                comp_quant((n - 1) % 4, (n - 1) // 4)
-
-        def e_quarter(n):
-            rt, jh = order[n]
-            for nb in range(4):
-                e_block(rt, 4 * jh + nb)
-
-        def z_unit(s, rt):
-            for th in range(2):
-                z_bank(s, rt, th)
-            z_group(s, rt)
-
-        comp_group(0, 0, 0, 4, "v")
+        comp_group(0)
+        permute_a()
         x_transpose(0)
-        for g in range(2):
-            a_permute(a_perm, a_raw, g, 4)
-            a_permute(as_perm, as_raw, g, 2)
-        e_quarter(0)
-        comp_step(1)
-        e_quarter(1)
-        comp_step(2)
-        nc.vector.tensor_copy(out=gain_sq[0:24, :], in_=gain_rows[:])
-        gain_bank = ps.tile([P, 4, P], F32, name="y_ps", bufs=2)
-        nc.tensor.transpose(gain_bank[:, 0, :], gain_sq[:], ident[:])
-        nc.vector.tensor_copy(out=gain_col[:], in_=gain_bank[:, 0, 0:24])
+        comp_quant(0)
+        e_blocks(0, 0)
+        e_blocks(0, 1)
         x_transpose(1)
-        comp_step(3)
-        e_quarter(2)
-        x_quant(0)
-        comp_step(4)
+        comp_group(1)
+        e_blocks(1, 0)
+        comp_quant(1)
+        comp_group(2)
         x_transpose(2)
+        e_quant(0)
+        e_blocks(1, 1)
         x_transpose(3)
-        comp_step(5)
-        z_unit(0, 0)
-        comp_step(6)
-        e_quarter(3)
-        e_quant(*order[0])
-        comp_step(7)
-        load_x(6)
-        load_x(7)
-        load_base(2)
-        load_base(3)
+        e_blocks(2, 0)
+        x_quant(0)
+        comp_quant(2)
+        e_blocks(2, 1)
+        e_blocks(3, 0)
         x_transpose(4)
-        e_quant(*order[1])
-        comp_step(8)
+        comp_group(3)
+        comp_group(4)
+        comp_group(5)
+        comp_quant(3)
+        comp_quant(4)
+        comp_quant(5)
+        gains_to_columns()
+        comp_group(6)
+        z_matmul(0, 0)
         x_transpose(5)
+        comp_group(7)
+        z_group(0, 0, nc.scalar.copy)
+        comp_quant(6)
+        comp_quant(7)
+        e_quant(1)
         x_quant(1)
-        z_unit(0, 1)
-        e_quant(*order[2])
-        z_quant(0, 0)
-        e_quant(*order[3])
-        z_unit(1, 0)
-        z_quant(0, 1)
+        e_blocks(3, 1)
         x_quant(2)
-
-        def y_unit(i, jh):
-            y_matmul(i, jh)
-            y_mult(i, jh)
-
-        banks = [(1, 1, 0), (1, 1, 1), (2, 0, 0), (2, 0, 1), (2, 1, 0), (2, 1, 1), (3, 0, 0), (3, 0, 1), (3, 1, 0), (3, 1, 1)]
-        units = [("d", i, jh) for i in range(4) for jh in range(2)]
-        units += [("d", 4, 0), ("d", 5, 0), ("t", 2, 1), ("t", 3, 0)]
-        units += [("b", i, (1, c)) for i in (4, 5) for c in range(C)]
-        units += [("t", 3, 1)]
-        units += [("b", i, (jh, c)) for jh in range(2) for i in (6, 7) for c in range(C)]
-        quants = {0: (1, 0), 1: (1, 1), 4: (2, 0), 6: (2, 1), 8: (3, 0), 9: (3, 1)}
-        pending = []
-        for n, (kind, i, jh) in enumerate(units):
-            if kind == "d":
-                y_unit(i, jh)
-            elif kind == "t":
-                yt_matmul(i, jh)
-            else:
-                yt_back(i, *jh)
-            for p in pending:
-                y_add(*p)
-            pending = [(i, jh)] if kind == "d" else []
-            if n in (2, 3):
-                x_transpose(4 + n)
-            if n == 4:
-                x_quant(3)
-            if n < len(banks):
-                z_bank(*banks[n])
-                if banks[n][2] == 1:
-                    z_group(*banks[n][:2])
-            if n in quants:
-                z_quant(*quants[n])
-            if n in (3, 5, 7, 8):
-                load_base(4 + (3, 5, 7, 8).index(n))
+        e_quant(2)
+        z_matmul(0, 1)
+        x_transpose(6)
+        e_quant(3)
+        z_group(0, 1, nc.vector.tensor_copy)
+        z_matmul(1, 0)
+        z_quant(0, 0)
+        z_quant(0, 1)
+        y_direct(0, 0)
+        z_group(1, 0, nc.scalar.copy)
+        y_direct(1, 0)
+        x_transpose(7)
+        add_base(0, 0)
+        z_matmul(2, 0)
+        x_quant(3)
+        z_quant(1, 0)
+        y_direct(0, 1)
+        z_group(2, 0, nc.scalar.copy)
+        z_matmul(1, 1)
+        z_group(1, 1, nc.scalar.copy)
+        add_base(1, 0)
+        z_quant(2, 0)
+        add_base(0, 1)
+        z_matmul(2, 1)
+        z_quant(1, 1)
+        z_group(2, 1, nc.scalar.copy)
+        y_direct(1, 1)
+        z_matmul(3, 1)
+        add_base(1, 1)
+        z_group(3, 1, nc.scalar.copy)
+        z_quant(2, 1)
+        y_direct(2, 0)
+        y_direct(3, 0)
+        y_transposed(2, 0)
+        add_base(2, 0)
+        y_direct(2, 1)
+        y_transposed(2, 1)
+        y_direct(3, 1)
+        turn_back(4, 0, 0)
+        z_matmul(3, 0)
+        add_base(3, 0)
+        turn_back(4, 0, 1)
+        turn_back(5, 0, 0)
+        z_group(3, 0, nc.scalar.copy)
+        z_quant(3, 1)
+        turn_back(5, 0, 1)
+        turn_back(4, 1, 0)
+        z_quant(3, 0)
+        turn_back(4, 1, 1)
+        turn_back(5, 1, 0)
+        add_base(2, 1)
+        y_transposed(3, 0)
+        turn_back(5, 1, 1)
+        add_base(3, 1)
+        turn_back(6, 0, 0)
+        y_transposed(3, 1)
+        turn_back(6, 0, 1)
+        turn_back(7, 0, 0)
+        turn_back(7, 0, 1)
+        turn_back(6, 1, 0)
+        turn_back(6, 1, 1)
+        turn_back(7, 1, 0)
+        turn_back(7, 1, 1)

@@ -8,98 +8,340 @@ BF16 = mybir.dt.bfloat16
 I32 = mybir.dt.int32
 U32 = mybir.dt.uint32
 U8 = mybir.dt.uint8
-FP8 = mybir.dt.float8_e4m3fn_x4
-FP4 = mybir.dt.float4_e2m1fn_x4
+MXFP8 = mybir.dt.float8_e4m3fn_x4
+MXFP4 = mybir.dt.float4_e2m1fn_x4
 ADD = mybir.AluOpType.add
 MULT = mybir.AluOpType.mult
 COPY = mybir.ActivationFunctionType.Copy
 
-L, K, R, N, C = 1024, 2048, 1024, 1024, 2
-FLOPS = 2 * L * K * R + 2 * R * R * N + 2 * L * R * N
+TOKENS, FEATURES, CHANNELS, COLUMNS, COPIES = 1024, 2048, 1024, 1024, 2
+FLOPS = 2 * TOKENS * FEATURES * CHANNELS + 2 * CHANNELS * CHANNELS * COLUMNS + 2 * TOKENS * CHANNELS * COLUMNS
 
 P = 128
-PASS = 512
-KG = K // PASS
-RT = R // PASS
-PAIR = 256
+WORD = 4
+PASS = P * WORD
+FEATURE_PASSES = FEATURES // PASS
+CHANNEL_PASSES = CHANNELS // PASS
+RUN = 8
+PAIR = 2 * P
+WORDS = PASS // 2
 HALF = 512
+BLOCKS = HALF // P
+SCALE_ROWS = 4
+GAIN_COLUMNS = CHANNELS // P
+GAIN_ROWS = GAIN_COLUMNS + COPIES * (COLUMNS // P)
 
 
-def tile_mora_repeated_update_s12_kernel(tc, x, comp, gain, a_words, a_scales, d_words, d_scales, copy_gain, base, out):
+def tile_mora_repeated_update_s12_kernel(
+    tc, x, comp, gain, a_words, a_scales, d_words, d_scales, copy_gain, base, out
+):
     nc = tc.nc
     with ExitStack() as ctx:
-        one = ctx.enter_context(tc.tile_pool(name="one", bufs=1))
-        sb = ctx.enter_context(tc.tile_pool(name="sb", bufs=2))
-        ps = ctx.enter_context(tc.psum_pool(name="ps", bufs=2))
+        resident = ctx.enter_context(tc.tile_pool(name="resident", bufs=1))
+        rotating = ctx.enter_context(tc.tile_pool(name="rotating", bufs=2))
+        psum = ctx.enter_context(tc.psum_pool(name="psum", bufs=2))
         ctx.enter_context(tc.manual_schedule())
 
-        a_raw = one.tile([P, 2, 2 * R], U8, name="a_raw", align_bytes=64)
-        a_perm = one.tile([P, 2, 2 * R], U8, name="a_perm", align_bytes=64)
-        a_scales_raw = one.tile([P, 2, R], U8, name="a_scales_raw", align_bytes=64)
-        a_scales_perm = one.tile([P, 2, R], U8, name="a_scales_perm", align_bytes=64)
-        d_sb = one.tile([P, 2, 2 * N], U8, name="d_sb", align_bytes=64)
-        d_scales_sb = one.tile([P, 2, N], U8, name="d_scales_sb", align_bytes=64)
-        comp_codes = one.tile([P, KG, R], U32, name="comp_codes", align_bytes=64)
-        comp_scales = one.tile([P, KG, R], U8, name="comp_scales", align_bytes=64)
-        e_codes = one.tile([P, RT, N], U32, name="e_codes", align_bytes=64)
-        e_scales = one.tile([P, RT, N], U8, name="e_scales", align_bytes=64)
-        cg = one.tile([P, C, N], BF16, name="cg", align_bytes=64)
-        ident = one.tile([P, P], F32, name="ident", align_bytes=64)
-        gain_rows = one.tile([24, P], BF16, name="gain_rows", align_bytes=64)
-        gain_sq = one.tile([P, P], F32, name="gain_sq", align_bytes=64)
-        gain_col = one.tile([P, 24], F32, name="gain_col", align_bytes=64)
-        warm = one.tile([P, 1], F32, name="warm", align_bytes=64)
+        a_codes_raw = resident.tile([P, CHANNEL_PASSES, 2 * CHANNELS], U8, name="a_codes_raw", align_bytes=64)
+        a_codes = resident.tile([P, CHANNEL_PASSES, 2 * CHANNELS], U8, name="a_codes", align_bytes=64)
+        d_codes = resident.tile([P, CHANNEL_PASSES, 2 * COLUMNS], U8, name="d_codes", align_bytes=64)
+        a_scales_raw = resident.tile([P, CHANNEL_PASSES, CHANNELS], U8, name="a_scales_raw", align_bytes=64)
+        a_scales_sb = resident.tile([P, CHANNEL_PASSES, CHANNELS], U8, name="a_scales_sb", align_bytes=64)
+        d_scales_sb = resident.tile([P, CHANNEL_PASSES, COLUMNS], U8, name="d_scales_sb", align_bytes=64)
+        comp_codes = resident.tile([P, FEATURE_PASSES, CHANNELS], U32, name="comp_codes", align_bytes=64)
+        comp_scales = resident.tile([P, FEATURE_PASSES, CHANNELS], U8, name="comp_scales", align_bytes=64)
+        e_codes = resident.tile([P, CHANNEL_PASSES, COLUMNS], U32, name="e_codes", align_bytes=64)
+        e_scales = resident.tile([P, CHANNEL_PASSES, COLUMNS], U8, name="e_scales", align_bytes=64)
+        copy_gain_sb = resident.tile([P, COPIES, COLUMNS], BF16, name="copy_gain_sb", align_bytes=64)
+        identity = resident.tile([P, P], F32, name="identity", align_bytes=64)
+        gain_rows = resident.tile([GAIN_ROWS, P], BF16, name="gain_rows", align_bytes=64)
+        gain_square = resident.tile([P, P], F32, name="gain_square", align_bytes=64)
+        gain_columns = resident.tile([P, GAIN_ROWS], F32, name="gain_columns", align_bytes=64)
+        dummy = resident.tile([P, 1], F32, name="dummy", align_bytes=64)
 
         nc.vector.memset(a_scales_raw[:].rearrange("p g n -> p (g n)").bitcast(I32), 0)
         nc.vector.memset(d_scales_sb[:].rearrange("p g n -> p (g n)").bitcast(I32), 0)
-        nc.vector.memset(warm[:], 0.0)
-        nc.vector.memset(gain_sq[:], 0.0)
-        make_identity(nc, ident[:])
-        nc.scalar.activation(out=warm[:], in_=warm[:], func=COPY)
+        nc.vector.memset(dummy[:], 0.0)
+        nc.vector.memset(gain_square[:], 0.0)
+        make_identity(nc, identity[:])
+        nc.scalar.activation(out=dummy[:], in_=dummy[:], func=COPY)
 
-        x_tiles, comp_raw, base_tiles = {}, {}, {}
+        x_rows, comp_rows, base_rows = {}, {}, {}
 
         def load_x(i):
-            x_tiles[i] = sb.tile([P, K], BF16, name="x_in", tag="token_rows", bufs=9, align_bytes=64)
-            nc.sync.dma_start(out=x_tiles[i][:], in_=x[P * i : P * (i + 1), :])
-
-        def load_comp(n):
-            rt, g = divmod(n, KG)
-            comp_raw[n] = sb.tile([P, 4, PASS], BF16, name="comp_raw", tag="half_block", bufs=8, align_bytes=64)
-            block = comp[PASS * g : PASS * (g + 1), PASS * rt : PASS * (rt + 1)]
-            nc.sync.dma_start(out=comp_raw[n][:], in_=block.rearrange("(p j) r -> p j r", j=4))
+            x_rows[i] = rotating.tile([P, FEATURES], BF16, name="x_rows", tag="token_rows", bufs=9, align_bytes=64)
+            nc.sync.dma_start(out=x_rows[i][:], in_=x[P * i : P * (i + 1), :])
 
         def load_base(i):
-            base_tiles[i] = sb.tile([P, C, N], BF16, name="base_in", tag="token_rows", bufs=9, align_bytes=64)
-            nc.sync.dma_start(out=base_tiles[i][:].rearrange("p c n -> p (c n)"), in_=base[P * i : P * (i + 1), :])
+            base_rows[i] = rotating.tile(
+                [P, COPIES, COLUMNS], BF16, name="base_rows", tag="token_rows", bufs=9, align_bytes=64
+            )
+            nc.sync.dma_start(out=base_rows[i][:].rearrange("p c n -> p (c n)"), in_=base[P * i : P * (i + 1), :])
 
-        def load_words(tile, src):
-            nc.sync.dma_start(out=tile[:].bitcast(I32), in_=src.rearrange("g p n -> p g n").bitcast(I32))
+        def load_comp(piece):
+            h, g = divmod(piece, FEATURE_PASSES)
+            comp_rows[piece] = rotating.tile(
+                [P, WORD, PASS], BF16, name="comp_rows", tag="four_kib", bufs=8, align_bytes=64
+            )
+            block = comp[PASS * g : PASS * (g + 1), PASS * h : PASS * (h + 1)]
+            nc.sync.dma_start(out=comp_rows[piece][:], in_=block.rearrange("(p v) r -> p v r", v=WORD))
 
-        def load_scales(tile, src):
-            for q in range(4):
+        def load_codes(tile, words):
+            nc.sync.dma_start(out=tile[:].bitcast(I32), in_=words.rearrange("g p n -> p g n").bitcast(I32))
+
+        def load_scales(tile, scales):
+            for quadrant in range(4):
+                rows = slice(SCALE_ROWS * quadrant, SCALE_ROWS * (quadrant + 1))
                 nc.sync.dma_start(
-                    out=tile[32 * q : 32 * q + 4, :, :].bitcast(I32),
-                    in_=src[:, 4 * q : 4 * q + 4, :].rearrange("g r n -> r g n").bitcast(I32),
+                    out=tile[32 * quadrant : 32 * quadrant + SCALE_ROWS, :, :].bitcast(I32),
+                    in_=scales[:, rows, :].rearrange("g r n -> r g n").bitcast(I32),
                 )
 
         def load_gains():
-            for rt in range(RT):
+            for h in range(CHANNEL_PASSES):
                 nc.sync.dma_start(
-                    out=gain_rows[4 * rt : 4 * rt + 4, :].rearrange("t (q e) -> t q e", e=8),
-                    in_=gain[PASS * rt : PASS * (rt + 1)].rearrange("(q t e) -> t q e", t=4, e=8),
+                    out=gain_rows[WORD * h : WORD * (h + 1), :].rearrange("t (q e) -> t q e", e=RUN),
+                    in_=gain[PASS * h : PASS * (h + 1)].rearrange("(q t e) -> t q e", t=WORD, e=RUN),
                 )
-            for c in range(C):
+            for c in range(COPIES):
+                first = GAIN_COLUMNS + c * (COLUMNS // P)
                 nc.sync.dma_start(
-                    out=gain_rows[8 + 8 * c : 16 + 8 * c, :],
+                    out=gain_rows[first : first + COLUMNS // P, :],
                     in_=copy_gain[c, :].rearrange("(b p) -> b p", p=P),
                 )
 
+        x_grouped, x_mx = {}, {}
+
+        def x_transpose(i):
+            s, place = divmod(i, 2)
+            if place == 0:
+                x_grouped[s] = rotating.tile([P, FEATURE_PASSES, PAIR, 2], F32, name="x_grouped", align_bytes=64)
+            words = x_rows[i][:].bitcast(F32)
+            for g0 in range(0, FEATURE_PASSES, 2):
+                bank = psum.tile([P, 4, P], F32, name="turned_ps", bufs=2)
+                for g in (g0, g0 + 1):
+                    for u in range(2):
+                        first = WORDS * g + u
+                        nc.tensor.transpose(bank[:, 2 * (g - g0) + u, :], words[:, first : first + WORDS - 1 : 2], identity[:])
+                nc.scalar.copy(
+                    out=x_grouped[s][:, g0 : g0 + 2, P * place : P * (place + 1), :],
+                    in_=bank[:].rearrange("p (g u) r -> p g r u", u=2),
+                )
+
+        def x_quantize(s):
+            codes = rotating.tile([P, FEATURE_PASSES, PAIR], U32, name="x_codes", bufs=3, align_bytes=64)
+            scales = rotating.tile([P, FEATURE_PASSES, PAIR], U8, name="x_scales", bufs=3, align_bytes=64)
+            nc.vector.quantize_mx(
+                out=codes[:].rearrange("p g r -> p (g r)").bitcast(MXFP8),
+                scales=scales[:].rearrange("p g r -> p (g r)"),
+                in_=x_grouped[s][:].rearrange("p g r u -> p (g r u)").bitcast(BF16),
+            )
+            x_mx[s] = (codes, scales)
+
+        comp_grouped = {}
+
+        def comp_group(piece):
+            comp_grouped[piece] = rotating.tile(
+                [P, WORD, P // RUN, RUN, WORD], BF16, name="comp_grouped", bufs=3, align_bytes=64
+            )
+            nc.vector.tensor_copy(
+                out=comp_grouped[piece][:],
+                in_=comp_rows[piece][:].rearrange("p v (q t e) -> p t q e v", t=WORD, e=RUN),
+            )
+
+        def comp_quantize(piece):
+            h, g = divmod(piece, FEATURE_PASSES)
+            columns = slice(PASS * h, PASS * (h + 1))
+            nc.vector.quantize_mx(
+                out=comp_codes[:, g, columns].bitcast(MXFP8),
+                scales=comp_scales[:, g, columns],
+                in_=comp_grouped[piece][:].rearrange("p t q e v -> p (t q e v)"),
+            )
+
+        def turn_gains():
+            nc.vector.tensor_copy(out=gain_square[0:GAIN_ROWS, :], in_=gain_rows[:])
+            bank = psum.tile([P, 4, P], F32, name="direct_ps", bufs=2)
+            nc.tensor.transpose(bank[:, 0, :], gain_square[:], identity[:])
+            nc.vector.tensor_copy(out=gain_columns[:], in_=bank[:, 0, 0:GAIN_ROWS])
+
+        e_grouped = {}
+
+        def permute_a():
+            for g in range(CHANNEL_PASSES):
+                for target, source, ints in ((a_codes, a_codes_raw, 4), (a_scales_sb, a_scales_raw, 2)):
+                    nc.vector.tensor_copy(
+                        out=target[:, g, :].bitcast(I32).rearrange(
+                            "p (h t q i) -> p h t q i", h=CHANNEL_PASSES, t=WORD, i=ints
+                        ),
+                        in_=source[:, g, :].bitcast(I32).rearrange(
+                            "p (h q t i) -> p h t q i", h=CHANNEL_PASSES, t=WORD, i=ints
+                        ),
+                    )
+
+        def e_matmul(part, side):
+            j, h = divmod(part, CHANNEL_PASSES)
+            if side == 0:
+                e_grouped[part] = rotating.tile([P, HALF, WORD], BF16, name="e_grouped", bufs=4, align_bytes=64)
+            for b in (2 * side, 2 * side + 1):
+                n = HALF * j + P * b
+                bank = psum.tile([P, WORD, P], F32, name="sums_ps", bufs=4)
+                for t in range(WORD):
+                    m = PASS * h + P * t
+                    for g in range(CHANNEL_PASSES):
+                        nc.tensor.matmul_mx(
+                            out=bank[:, t, :],
+                            lhsT=a_codes[:, g, 2 * m : 2 * (m + P)].bitcast(MXFP4),
+                            lhsT_scale=a_scales_sb[:, g, m : m + P],
+                            rhs=d_codes[:, g, 2 * n : 2 * (n + P)].bitcast(MXFP4),
+                            rhs_scale=d_scales_sb[:, g, n : n + P],
+                            start=(g == 0),
+                            stop=(g == CHANNEL_PASSES - 1),
+                        )
+                nc.scalar.copy(
+                    out=e_grouped[part][:, P * b : P * (b + 1), :], in_=bank[:].rearrange("p t n -> p n t")
+                )
+
+        def e_quantize(part):
+            j, h = divmod(part, CHANNEL_PASSES)
+            columns = slice(HALF * j, HALF * (j + 1))
+            nc.vector.quantize_mx(
+                out=e_codes[:, h, columns].bitcast(MXFP8),
+                scales=e_scales[:, h, columns],
+                in_=e_grouped[part][:].rearrange("p n t -> p (n t)"),
+            )
+
+        z_rounded, z_grouped, z_mx = {}, {}, {}
+
+        def z_matmul(s, h):
+            codes, scales = x_mx[s]
+            z_rounded[(s, h)] = rotating.tile([P, WORD, PAIR], BF16, name="z_rounded", bufs=3, align_bytes=64)
+            for i in range(WORD // 2):
+                bank = psum.tile([P, 2, PAIR], F32, name="sums_ps", bufs=4)
+                for t in (2 * i, 2 * i + 1):
+                    m = PASS * h + P * t
+                    for g in range(FEATURE_PASSES):
+                        nc.tensor.matmul_mx(
+                            out=bank[:, t - 2 * i, :],
+                            lhsT=comp_codes[:, g, m : m + P].bitcast(MXFP8),
+                            lhsT_scale=comp_scales[:, g, m : m + P],
+                            rhs=codes[:, g, :].bitcast(MXFP8),
+                            rhs_scale=scales[:, g, :],
+                            start=(g == 0),
+                            stop=(g == FEATURE_PASSES - 1),
+                        )
+                for t in (2 * i, 2 * i + 1):
+                    column = WORD * h + t
+                    nc.scalar.activation(
+                        out=z_rounded[(s, h)][:, t, :],
+                        in_=bank[:, t - 2 * i, :],
+                        func=COPY,
+                        scale=gain_columns[:, column : column + 1],
+                    )
+
+        def z_group(s, h, copy):
+            z_grouped[(s, h)] = rotating.tile([P, PAIR, WORD], BF16, name="z_grouped", bufs=4, align_bytes=64)
+            copy(
+                out=z_grouped[(s, h)][:].rearrange("p (k i) t -> p k t i", i=4),
+                in_=z_rounded[(s, h)][:].rearrange("p t (k i) -> p k t i", i=4),
+            )
+
+        def z_quantize(s, h):
+            codes = rotating.tile([P, PAIR], U32, name="z_codes", bufs=8, align_bytes=64)
+            scales = rotating.tile([P, PAIR], U8, name="z_scales", bufs=8, align_bytes=64)
+            nc.vector.quantize_mx(
+                out=codes[:].bitcast(MXFP8),
+                scales=scales[:],
+                in_=z_grouped[(s, h)][:].rearrange("p r t -> p (r t)"),
+            )
+            z_mx[(s, h)] = (codes, scales)
+
+        products = {}
+
+        def y_direct(i, j):
+            s, place = divmod(i, 2)
+            columns = slice(HALF * j, HALF * (j + 1))
+            bank = psum.tile([P, HALF], F32, name="direct_ps", bufs=2)
+            for h in range(CHANNEL_PASSES):
+                codes, scales = z_mx[(s, h)]
+                nc.tensor.matmul_mx(
+                    out=bank[:],
+                    lhsT=codes[:, P * place : P * (place + 1)].bitcast(MXFP8),
+                    lhsT_scale=scales[:, P * place : P * (place + 1)],
+                    rhs=e_codes[:, h, columns].bitcast(MXFP8),
+                    rhs_scale=e_scales[:, h, columns],
+                    start=(h == 0),
+                    stop=(h == CHANNEL_PASSES - 1),
+                )
+            products[(i, j)] = rotating.tile(
+                [P, COPIES, HALF], F32, name="product", tag="four_kib", bufs=8, align_bytes=64
+            )
+            nc.vector.tensor_tensor(
+                out=products[(i, j)][:],
+                in0=bank[:].unsqueeze(1).to_broadcast([P, COPIES, HALF]),
+                in1=copy_gain_sb[:, :, columns],
+                op=MULT,
+            )
+
+        def add_base(i, j):
+            columns = slice(HALF * j, HALF * (j + 1))
+            product = products[(i, j)]
+            nc.vector.tensor_tensor(out=product[:], in0=product[:], in1=base_rows[i][:, :, columns], op=ADD)
+            rows = out[P * i : P * (i + 1), :].rearrange("p (c n) -> p c n", c=COPIES)
+            nc.sync.dma_start(out=rows[:, :, columns], in_=product[:])
+
+        turned_products = {}
+
+        def y_transposed(s, j):
+            banks = []
+            for b in range(BLOCKS):
+                if b % 2 == 0:
+                    banks.append(psum.tile([P, 2, PAIR], F32, name="sums_ps", bufs=4))
+                columns = slice(HALF * j + P * b, HALF * j + P * (b + 1))
+                for h in range(CHANNEL_PASSES):
+                    codes, scales = z_mx[(s, h)]
+                    nc.tensor.matmul_mx(
+                        out=banks[b // 2][:, b % 2, :],
+                        lhsT=e_codes[:, h, columns].bitcast(MXFP8),
+                        lhsT_scale=e_scales[:, h, columns],
+                        rhs=codes[:].bitcast(MXFP8),
+                        rhs_scale=scales[:],
+                        start=(h == 0),
+                        stop=(h == CHANNEL_PASSES - 1),
+                    )
+            turned = rotating.tile([P, COPIES, BLOCKS, PAIR], F32, name="turned", align_bytes=64)
+            for c in range(COPIES):
+                for b in range(BLOCKS):
+                    column = GAIN_COLUMNS + c * (COLUMNS // P) + BLOCKS * j + b
+                    nc.scalar.activation(
+                        out=turned[:, c, b, :],
+                        in_=banks[b // 2][:, b % 2, :],
+                        func=COPY,
+                        scale=gain_columns[:, column : column + 1],
+                    )
+            turned_products[(s, j)] = turned
+
+        def turn_back(i, j, c):
+            s, place = divmod(i, 2)
+            bank = psum.tile([P, BLOCKS, P], F32, name="turned_ps", bufs=2)
+            for b in range(BLOCKS):
+                nc.tensor.transpose(
+                    bank[:, b, :], turned_products[(s, j)][:, c, b, P * place : P * (place + 1)], identity[:]
+                )
+            total = rotating.tile([P, HALF], F32, name="total", bufs=8, align_bytes=64)
+            nc.vector.tensor_tensor(
+                out=total[:],
+                in0=bank[:].rearrange("p b n -> p (b n)"),
+                in1=base_rows[i][:, c, HALF * j : HALF * (j + 1)],
+                op=ADD,
+            )
+            first = COLUMNS * c + HALF * j
+            nc.sync.dma_start(out=out[P * i : P * (i + 1), first : first + HALF], in_=total[:])
+
         load_comp(0)
-        load_x(0)
-        load_words(a_raw, a_words)
-        load_words(d_sb, d_words)
         load_scales(a_scales_raw, a_scales)
+        load_x(0)
+        load_codes(a_codes_raw, a_words)
+        load_codes(d_codes, d_words)
         load_scales(d_scales_sb, d_scales)
         load_comp(1)
         load_x(1)
@@ -107,279 +349,92 @@ def tile_mora_repeated_update_s12_kernel(tc, x, comp, gain, a_words, a_scales, d
         load_x(2)
         load_gains()
         load_x(3)
-        for n in range(3, 7):
-            load_comp(n)
+        for piece in range(3, 7):
+            load_comp(piece)
         load_x(4)
         load_comp(7)
-        load_x(5)
-        load_x(6)
-        load_x(7)
-        nc.sync.dma_start(out=cg[:].rearrange("p c n -> p (c n)"), in_=copy_gain.rearrange("c n -> (c n)").partition_broadcast(P))
-        for i in range(8):
+        for i in range(5, 8):
+            load_x(i)
+        nc.sync.dma_start(
+            out=copy_gain_sb[:].rearrange("p c n -> p (c n)"),
+            in_=copy_gain.rearrange("c n -> (c n)").partition_broadcast(P),
+        )
+        for i in range(TOKENS // P):
             load_base(i)
-
-        xg, x_codes = {}, {}
-
-        def x_transpose(i):
-            s, h = divmod(i, 2)
-            if h == 0:
-                xg[s] = sb.tile([P, KG, PAIR, 2], F32, name="xg", align_bytes=64)
-            words = x_tiles[i][:].bitcast(F32)
-            for b in range(2):
-                bank = ps.tile([P, 4, P], F32, name="xt_ps", bufs=2)
-                for g2 in range(2):
-                    for u in range(2):
-                        w0 = 256 * (2 * b + g2) + u
-                        nc.tensor.transpose(bank[:, 2 * g2 + u, :], words[:, w0 : w0 + 255 : 2], ident[:])
-                nc.scalar.copy(
-                    out=xg[s][:, 2 * b : 2 * b + 2, P * h : P * (h + 1), :],
-                    in_=bank[:].rearrange("p (g u) r -> p g r u", u=2),
-                )
-
-        def x_quant(s):
-            codes = sb.tile([P, KG, PAIR], U32, name="x_codes", bufs=3, align_bytes=64)
-            scales = sb.tile([P, KG, PAIR], U8, name="x_scales", bufs=3, align_bytes=64)
-            nc.vector.quantize_mx(
-                out=codes[:].rearrange("p g r -> p (g r)").bitcast(FP8),
-                scales=scales[:].rearrange("p g r -> p (g r)"),
-                in_=xg[s][:].rearrange("p g r u -> p (g r u)").bitcast(BF16),
-            )
-            x_codes[s] = (codes, scales)
-
-        comp_grouped = {}
-
-        def comp_group(n):
-            comp_grouped[n] = sb.tile([P, 4, 16, 8, 4], BF16, name="comp_grouped", bufs=3, align_bytes=64)
-            nc.vector.tensor_copy(
-                out=comp_grouped[n][:],
-                in_=comp_raw[n][:].rearrange("p j (q t e) -> p t q e j", t=4, e=8),
-            )
-
-        def comp_quant(n):
-            rt, g = divmod(n, KG)
-            cols = slice(PASS * rt, PASS * (rt + 1))
-            nc.vector.quantize_mx(
-                out=comp_codes[:, g, cols].bitcast(FP8),
-                scales=comp_scales[:, g, cols],
-                in_=comp_grouped[n][:].rearrange("p t q e j -> p (t q e j)"),
-            )
-
-        def gains_to_columns():
-            nc.vector.tensor_copy(out=gain_sq[0:24, :], in_=gain_rows[:])
-            bank = ps.tile([P, 4, P], F32, name="y_ps", bufs=2)
-            nc.tensor.transpose(bank[:, 0, :], gain_sq[:], ident[:])
-            nc.vector.tensor_copy(out=gain_col[:], in_=bank[:, 0, 0:24])
-
-        eg = {}
-
-        def permute_a():
-            for g in range(2):
-                for dst, src, w in ((a_perm, a_raw, 4), (a_scales_perm, a_scales_raw, 2)):
-                    nc.vector.tensor_copy(
-                        out=dst[:, g, :].bitcast(I32).rearrange("p (r t q w) -> p r t q w", r=RT, t=4, w=w),
-                        in_=src[:, g, :].bitcast(I32).rearrange("p (r q t w) -> p r t q w", r=RT, t=4, w=w),
-                    )
-
-        def e_blocks(quarter, half):
-            jh, rt = divmod(quarter, RT)
-            if half == 0:
-                eg[quarter] = sb.tile([P, HALF, 4], BF16, name="eg", bufs=4, align_bytes=64)
-            for b in (2 * half, 2 * half + 1):
-                nb = 4 * jh + b
-                bank = ps.tile([P, 4, P], F32, name="acc_ps", bufs=4)
-                for t in range(4):
-                    col = PASS * rt + P * t
-                    for g in range(2):
-                        nc.tensor.matmul_mx(
-                            out=bank[:, t, :],
-                            lhsT=a_perm[:, g, 2 * col : 2 * (col + P)].bitcast(FP4),
-                            lhsT_scale=a_scales_perm[:, g, col : col + P],
-                            rhs=d_sb[:, g, 2 * P * nb : 2 * P * (nb + 1)].bitcast(FP4),
-                            rhs_scale=d_scales_sb[:, g, P * nb : P * (nb + 1)],
-                            start=(g == 0),
-                            stop=(g == 1),
-                        )
-                nc.scalar.copy(out=eg[quarter][:, P * b : P * (b + 1), :], in_=bank[:].rearrange("p t n -> p n t"))
-
-        def e_quant(quarter):
-            jh, rt = divmod(quarter, RT)
-            cols = slice(HALF * jh, HALF * (jh + 1))
-            nc.vector.quantize_mx(
-                out=e_codes[:, rt, cols].bitcast(FP8),
-                scales=e_scales[:, rt, cols],
-                in_=eg[quarter][:].rearrange("p n t -> p (n t)"),
-            )
-
-        zc, zg, z_codes = {}, {}, {}
-
-        def z_matmul(s, rt):
-            codes, scales = x_codes[s]
-            zc[(s, rt)] = sb.tile([P, 4, PAIR], BF16, name="zc", bufs=3, align_bytes=64)
-            for th in range(2):
-                bank = ps.tile([P, 2, PAIR], F32, name="acc_ps", bufs=4)
-                for h in range(2):
-                    col = PASS * rt + P * (2 * th + h)
-                    for g in range(KG):
-                        nc.tensor.matmul_mx(
-                            out=bank[:, h, :],
-                            lhsT=comp_codes[:, g, col : col + P].bitcast(FP8),
-                            lhsT_scale=comp_scales[:, g, col : col + P],
-                            rhs=codes[:, g, :].bitcast(FP8),
-                            rhs_scale=scales[:, g, :],
-                            start=(g == 0),
-                            stop=(g == KG - 1),
-                        )
-                for h in range(2):
-                    t = 2 * th + h
-                    k = 4 * rt + t
-                    nc.scalar.activation(out=zc[(s, rt)][:, t, :], in_=bank[:, h, :], func=COPY, scale=gain_col[:, k : k + 1])
-
-        def z_group(s, rt, copy):
-            zg[(s, rt)] = sb.tile([P, PAIR, 4], BF16, name="zg", bufs=4, align_bytes=64)
-            copy(out=zg[(s, rt)][:], in_=zc[(s, rt)][:].rearrange("p t r -> p r t"))
-
-        def z_quant(s, rt):
-            codes = sb.tile([P, PAIR], U32, name="z_codes", bufs=8, align_bytes=64)
-            scales = sb.tile([P, PAIR], U8, name="z_scales", bufs=8, align_bytes=64)
-            nc.vector.quantize_mx(out=codes[:].bitcast(FP8), scales=scales[:], in_=zg[(s, rt)][:].rearrange("p r t -> p (r t)"))
-            z_codes[(s, rt)] = (codes, scales)
-
-        products, yt = {}, {}
-
-        def y_direct(i, jh):
-            s, h = divmod(i, 2)
-            cols = slice(HALF * jh, HALF * (jh + 1))
-            bank = ps.tile([P, HALF], F32, name="y_ps", bufs=2)
-            for rt in range(RT):
-                codes, scales = z_codes[(s, rt)]
-                nc.tensor.matmul_mx(
-                    out=bank[:],
-                    lhsT=codes[:, P * h : P * (h + 1)].bitcast(FP8),
-                    lhsT_scale=scales[:, P * h : P * (h + 1)],
-                    rhs=e_codes[:, rt, cols].bitcast(FP8),
-                    rhs_scale=e_scales[:, rt, cols],
-                    start=(rt == 0),
-                    stop=(rt == RT - 1),
-                )
-            products[(i, jh)] = sb.tile([P, C, HALF], F32, name="product", tag="half_block", bufs=8, align_bytes=64)
-            nc.vector.tensor_tensor(
-                out=products[(i, jh)][:],
-                in0=bank[:].unsqueeze(1).to_broadcast([P, C, HALF]),
-                in1=cg[:, :, cols],
-                op=MULT,
-            )
-
-        def add_base(i, jh):
-            cols = slice(HALF * jh, HALF * (jh + 1))
-            product = products[(i, jh)]
-            nc.vector.tensor_tensor(out=product[:], in0=product[:], in1=base_tiles[i][:, :, cols], op=ADD)
-            nc.sync.dma_start(out=out[P * i : P * (i + 1), :].rearrange("p (c n) -> p c n", c=C)[:, :, cols], in_=product[:])
-
-        def y_transposed(s, jh):
-            banks = []
-            for b in range(4):
-                if b % 2 == 0:
-                    banks.append(ps.tile([P, 2, PAIR], F32, name="acc_ps", bufs=4))
-                cols = slice(HALF * jh + P * b, HALF * jh + P * (b + 1))
-                for rt in range(RT):
-                    codes, scales = z_codes[(s, rt)]
-                    nc.tensor.matmul_mx(
-                        out=banks[b // 2][:, b % 2, :],
-                        lhsT=e_codes[:, rt, cols].bitcast(FP8),
-                        lhsT_scale=e_scales[:, rt, cols],
-                        rhs=codes[:].bitcast(FP8),
-                        rhs_scale=scales[:],
-                        start=(rt == 0),
-                        stop=(rt == RT - 1),
-                    )
-            yt[(s, jh)] = sb.tile([P, C, 4, PAIR], F32, name="yt", align_bytes=64)
-            for c in range(C):
-                for b in range(4):
-                    k = 8 + 8 * c + 4 * jh + b
-                    nc.scalar.activation(out=yt[(s, jh)][:, c, b, :], in_=banks[b // 2][:, b % 2, :], func=COPY, scale=gain_col[:, k : k + 1])
-
-        def turn_back(i, jh, c):
-            s, h = divmod(i, 2)
-            bank = ps.tile([P, 4, P], F32, name="xt_ps", bufs=2)
-            for b in range(4):
-                nc.tensor.transpose(bank[:, b, :], yt[(s, jh)][:, c, b, P * h : P * (h + 1)], ident[:])
-            quarter = sb.tile([P, HALF], F32, name="quarter", bufs=8, align_bytes=64)
-            cols = slice(HALF * jh, HALF * (jh + 1))
-            nc.vector.tensor_tensor(out=quarter[:], in0=bank[:].rearrange("p b t -> p (b t)"), in1=base_tiles[i][:, c, cols], op=ADD)
-            nc.sync.dma_start(out=out[P * i : P * (i + 1), N * c + HALF * jh : N * c + HALF * (jh + 1)], in_=quarter[:])
 
         comp_group(0)
         permute_a()
         x_transpose(0)
-        comp_quant(0)
-        e_blocks(0, 0)
-        e_blocks(0, 1)
+        comp_quantize(0)
+        e_matmul(0, 0)
+        e_matmul(0, 1)
         x_transpose(1)
         comp_group(1)
-        e_blocks(1, 0)
-        comp_quant(1)
+        e_matmul(1, 0)
+        comp_quantize(1)
         comp_group(2)
         x_transpose(2)
-        e_quant(0)
-        e_blocks(1, 1)
+        e_quantize(0)
+        e_matmul(1, 1)
         x_transpose(3)
-        e_blocks(2, 0)
-        x_quant(0)
-        comp_quant(2)
-        e_blocks(2, 1)
-        e_blocks(3, 0)
+        e_matmul(2, 0)
+        x_quantize(0)
+        comp_quantize(2)
+        e_matmul(2, 1)
+        e_matmul(3, 0)
         x_transpose(4)
-        comp_group(3)
-        comp_group(4)
-        comp_group(5)
-        comp_quant(3)
-        comp_quant(4)
-        comp_quant(5)
-        gains_to_columns()
+        for piece in range(3, 6):
+            comp_group(piece)
+        for piece in range(3, 6):
+            comp_quantize(piece)
+
+        turn_gains()
         comp_group(6)
         z_matmul(0, 0)
         x_transpose(5)
         comp_group(7)
         z_group(0, 0, nc.scalar.copy)
-        comp_quant(6)
-        comp_quant(7)
-        e_quant(1)
-        x_quant(1)
-        e_blocks(3, 1)
-        x_quant(2)
-        e_quant(2)
+        comp_quantize(6)
+        comp_quantize(7)
+        e_quantize(1)
+        x_quantize(1)
+        e_matmul(3, 1)
+        x_quantize(2)
+        e_quantize(2)
         z_matmul(0, 1)
         x_transpose(6)
-        e_quant(3)
+        e_quantize(3)
         z_group(0, 1, nc.vector.tensor_copy)
         z_matmul(1, 0)
-        z_quant(0, 0)
-        z_quant(0, 1)
+        z_quantize(0, 0)
+        z_quantize(0, 1)
+
         y_direct(0, 0)
         z_group(1, 0, nc.scalar.copy)
         y_direct(1, 0)
         x_transpose(7)
         add_base(0, 0)
         z_matmul(2, 0)
-        x_quant(3)
-        z_quant(1, 0)
+        x_quantize(3)
+        z_quantize(1, 0)
         y_direct(0, 1)
         z_group(2, 0, nc.scalar.copy)
         z_matmul(1, 1)
         z_group(1, 1, nc.scalar.copy)
         add_base(1, 0)
-        z_quant(2, 0)
+        z_quantize(2, 0)
         add_base(0, 1)
         z_matmul(2, 1)
-        z_quant(1, 1)
+        z_quantize(1, 1)
         z_group(2, 1, nc.scalar.copy)
         y_direct(1, 1)
         z_matmul(3, 1)
         add_base(1, 1)
         z_group(3, 1, nc.scalar.copy)
-        z_quant(2, 1)
+        z_quantize(2, 1)
         y_direct(2, 0)
         y_direct(3, 0)
+
         y_transposed(2, 0)
         add_base(2, 0)
         y_direct(2, 1)
@@ -391,16 +446,17 @@ def tile_mora_repeated_update_s12_kernel(tc, x, comp, gain, a_words, a_scales, d
         turn_back(4, 0, 1)
         turn_back(5, 0, 0)
         z_group(3, 0, nc.scalar.copy)
-        z_quant(3, 1)
+        z_quantize(3, 1)
         turn_back(5, 0, 1)
         turn_back(4, 1, 0)
-        z_quant(3, 0)
+        z_quantize(3, 0)
         turn_back(4, 1, 1)
         turn_back(5, 1, 0)
         add_base(2, 1)
         y_transposed(3, 0)
         turn_back(5, 1, 1)
         add_base(3, 1)
+
         turn_back(6, 0, 0)
         y_transposed(3, 1)
         turn_back(6, 0, 1)

from contextlib import ExitStack

import concourse.mybir as mybir
from concourse.masks import make_identity

F32 = mybir.dt.float32
BF16 = mybir.dt.bfloat16
I32 = mybir.dt.int32
U32 = mybir.dt.uint32
U8 = mybir.dt.uint8
MXFP8 = mybir.dt.float8_e4m3fn_x4
MXFP4 = mybir.dt.float4_e2m1fn_x4
ADD = mybir.AluOpType.add
MULT = mybir.AluOpType.mult
COPY = mybir.ActivationFunctionType.Copy

TOKENS, FEATURES, CHANNELS, COLUMNS, COPIES = 1024, 2048, 1024, 1024, 2
FLOPS = 2 * TOKENS * FEATURES * CHANNELS + 2 * CHANNELS * CHANNELS * COLUMNS + 2 * TOKENS * CHANNELS * COLUMNS

P = 128
WORD = 4
PASS = P * WORD
FEATURE_PASSES = FEATURES // PASS
CHANNEL_PASSES = CHANNELS // PASS
RUN = 8
PAIR = 2 * P
WORDS = PASS // 2
HALF = 512
BLOCKS = HALF // P
SCALE_ROWS = 4
GAIN_COLUMNS = CHANNELS // P
GAIN_ROWS = GAIN_COLUMNS + COPIES * (COLUMNS // P)


def tile_mora_repeated_update_s12_kernel(
    tc, x, comp, gain, a_words, a_scales, d_words, d_scales, copy_gain, base, out
):
    nc = tc.nc
    with ExitStack() as ctx:
        resident = ctx.enter_context(tc.tile_pool(name="resident", bufs=1))
        rotating = ctx.enter_context(tc.tile_pool(name="rotating", bufs=2))
        psum = ctx.enter_context(tc.psum_pool(name="psum", bufs=2))
        ctx.enter_context(tc.manual_schedule())

        a_codes_raw = resident.tile([P, CHANNEL_PASSES, 2 * CHANNELS], U8, name="a_codes_raw", align_bytes=64)
        a_codes = resident.tile([P, CHANNEL_PASSES, 2 * CHANNELS], U8, name="a_codes", align_bytes=64)
        d_codes = resident.tile([P, CHANNEL_PASSES, 2 * COLUMNS], U8, name="d_codes", align_bytes=64)
        a_scales_raw = resident.tile([P, CHANNEL_PASSES, CHANNELS], U8, name="a_scales_raw", align_bytes=64)
        a_scales_sb = resident.tile([P, CHANNEL_PASSES, CHANNELS], U8, name="a_scales_sb", align_bytes=64)
        d_scales_sb = resident.tile([P, CHANNEL_PASSES, COLUMNS], U8, name="d_scales_sb", align_bytes=64)
        comp_codes = resident.tile([P, FEATURE_PASSES, CHANNELS], U32, name="comp_codes", align_bytes=64)
        comp_scales = resident.tile([P, FEATURE_PASSES, CHANNELS], U8, name="comp_scales", align_bytes=64)
        e_codes = resident.tile([P, CHANNEL_PASSES, COLUMNS], U32, name="e_codes", align_bytes=64)
        e_scales = resident.tile([P, CHANNEL_PASSES, COLUMNS], U8, name="e_scales", align_bytes=64)
        copy_gain_sb = resident.tile([P, COPIES, COLUMNS], BF16, name="copy_gain_sb", align_bytes=64)
        identity = resident.tile([P, P], F32, name="identity", align_bytes=64)
        gain_rows = resident.tile([GAIN_ROWS, P], BF16, name="gain_rows", align_bytes=64)
        gain_square = resident.tile([P, P], F32, name="gain_square", align_bytes=64)
        gain_columns = resident.tile([P, GAIN_ROWS], F32, name="gain_columns", align_bytes=64)
        dummy = resident.tile([P, 1], F32, name="dummy", align_bytes=64)

        nc.vector.memset(a_scales_raw[:].rearrange("p g n -> p (g n)").bitcast(I32), 0)
        nc.vector.memset(d_scales_sb[:].rearrange("p g n -> p (g n)").bitcast(I32), 0)
        nc.vector.memset(dummy[:], 0.0)
        nc.vector.memset(gain_square[:], 0.0)
        make_identity(nc, identity[:])
        nc.scalar.activation(out=dummy[:], in_=dummy[:], func=COPY)

        x_rows, comp_rows, base_rows = {}, {}, {}

        def load_x(i):
            x_rows[i] = rotating.tile([P, FEATURES], BF16, name="x_rows", tag="token_rows", bufs=9, align_bytes=64)
            nc.sync.dma_start(out=x_rows[i][:], in_=x[P * i : P * (i + 1), :])

        def load_base(i):
            base_rows[i] = rotating.tile(
                [P, COPIES, COLUMNS], BF16, name="base_rows", tag="token_rows", bufs=9, align_bytes=64
            )
            nc.sync.dma_start(out=base_rows[i][:].rearrange("p c n -> p (c n)"), in_=base[P * i : P * (i + 1), :])

        def load_comp(piece):
            h, g = divmod(piece, FEATURE_PASSES)
            comp_rows[piece] = rotating.tile(
                [P, WORD, PASS], BF16, name="comp_rows", tag="four_kib", bufs=8, align_bytes=64
            )
            block = comp[PASS * g : PASS * (g + 1), PASS * h : PASS * (h + 1)]
            nc.sync.dma_start(out=comp_rows[piece][:], in_=block.rearrange("(p v) r -> p v r", v=WORD))

        def load_codes(tile, words):
            nc.sync.dma_start(out=tile[:].bitcast(I32), in_=words.rearrange("g p n -> p g n").bitcast(I32))

        def load_scales(tile, scales):
            for quadrant in range(4):
                rows = slice(SCALE_ROWS * quadrant, SCALE_ROWS * (quadrant + 1))
                nc.sync.dma_start(
                    out=tile[32 * quadrant : 32 * quadrant + SCALE_ROWS, :, :].bitcast(I32),
                    in_=scales[:, rows, :].rearrange("g r n -> r g n").bitcast(I32),
                )

        def load_gains():
            for h in range(CHANNEL_PASSES):
                nc.sync.dma_start(
                    out=gain_rows[WORD * h : WORD * (h + 1), :].rearrange("t (q e) -> t q e", e=RUN),
                    in_=gain[PASS * h : PASS * (h + 1)].rearrange("(q t e) -> t q e", t=WORD, e=RUN),
                )
            for c in range(COPIES):
                first = GAIN_COLUMNS + c * (COLUMNS // P)
                nc.sync.dma_start(
                    out=gain_rows[first : first + COLUMNS // P, :],
                    in_=copy_gain[c, :].rearrange("(b p) -> b p", p=P),
                )

        x_grouped, x_mx = {}, {}

        def x_transpose(i):
            s, place = divmod(i, 2)
            if place == 0:
                x_grouped[s] = rotating.tile([P, FEATURE_PASSES, PAIR, 2], F32, name="x_grouped", align_bytes=64)
            words = x_rows[i][:].bitcast(F32)
            for g0 in range(0, FEATURE_PASSES, 2):
                bank = psum.tile([P, 4, P], F32, name="turned_ps", bufs=2)
                for g in (g0, g0 + 1):
                    for u in range(2):
                        first = WORDS * g + u
                        nc.tensor.transpose(bank[:, 2 * (g - g0) + u, :], words[:, first : first + WORDS - 1 : 2], identity[:])
                nc.scalar.copy(
                    out=x_grouped[s][:, g0 : g0 + 2, P * place : P * (place + 1), :],
                    in_=bank[:].rearrange("p (g u) r -> p g r u", u=2),
                )

        def x_quantize(s):
            codes = rotating.tile([P, FEATURE_PASSES, PAIR], U32, name="x_codes", bufs=3, align_bytes=64)
            scales = rotating.tile([P, FEATURE_PASSES, PAIR], U8, name="x_scales", bufs=3, align_bytes=64)
            nc.vector.quantize_mx(
                out=codes[:].rearrange("p g r -> p (g r)").bitcast(MXFP8),
                scales=scales[:].rearrange("p g r -> p (g r)"),
                in_=x_grouped[s][:].rearrange("p g r u -> p (g r u)").bitcast(BF16),
            )
            x_mx[s] = (codes, scales)

        comp_grouped = {}

        def comp_group(piece):
            comp_grouped[piece] = rotating.tile(
                [P, WORD, P // RUN, RUN, WORD], BF16, name="comp_grouped", bufs=3, align_bytes=64
            )
            nc.vector.tensor_copy(
                out=comp_grouped[piece][:],
                in_=comp_rows[piece][:].rearrange("p v (q t e) -> p t q e v", t=WORD, e=RUN),
            )

        def comp_quantize(piece):
            h, g = divmod(piece, FEATURE_PASSES)
            columns = slice(PASS * h, PASS * (h + 1))
            nc.vector.quantize_mx(
                out=comp_codes[:, g, columns].bitcast(MXFP8),
                scales=comp_scales[:, g, columns],
                in_=comp_grouped[piece][:].rearrange("p t q e v -> p (t q e v)"),
            )

        def turn_gains():
            nc.vector.tensor_copy(out=gain_square[0:GAIN_ROWS, :], in_=gain_rows[:])
            bank = psum.tile([P, 4, P], F32, name="direct_ps", bufs=2)
            nc.tensor.transpose(bank[:, 0, :], gain_square[:], identity[:])
            nc.vector.tensor_copy(out=gain_columns[:], in_=bank[:, 0, 0:GAIN_ROWS])

        e_grouped = {}

        def permute_a():
            for g in range(CHANNEL_PASSES):
                for target, source, ints in ((a_codes, a_codes_raw, 4), (a_scales_sb, a_scales_raw, 2)):
                    nc.vector.tensor_copy(
                        out=target[:, g, :].bitcast(I32).rearrange(
                            "p (h t q i) -> p h t q i", h=CHANNEL_PASSES, t=WORD, i=ints
                        ),
                        in_=source[:, g, :].bitcast(I32).rearrange(
                            "p (h q t i) -> p h t q i", h=CHANNEL_PASSES, t=WORD, i=ints
                        ),
                    )

        def e_matmul(part, side):
            j, h = divmod(part, CHANNEL_PASSES)
            if side == 0:
                e_grouped[part] = rotating.tile([P, HALF, WORD], BF16, name="e_grouped", bufs=4, align_bytes=64)
            for b in (2 * side, 2 * side + 1):
                n = HALF * j + P * b
                bank = psum.tile([P, WORD, P], F32, name="sums_ps", bufs=4)
                for t in range(WORD):
                    m = PASS * h + P * t
                    for g in range(CHANNEL_PASSES):
                        nc.tensor.matmul_mx(
                            out=bank[:, t, :],
                            lhsT=a_codes[:, g, 2 * m : 2 * (m + P)].bitcast(MXFP4),
                            lhsT_scale=a_scales_sb[:, g, m : m + P],
                            rhs=d_codes[:, g, 2 * n : 2 * (n + P)].bitcast(MXFP4),
                            rhs_scale=d_scales_sb[:, g, n : n + P],
                            start=(g == 0),
                            stop=(g == CHANNEL_PASSES - 1),
                        )
                nc.scalar.copy(
                    out=e_grouped[part][:, P * b : P * (b + 1), :], in_=bank[:].rearrange("p t n -> p n t")
                )

        def e_quantize(part):
            j, h = divmod(part, CHANNEL_PASSES)
            columns = slice(HALF * j, HALF * (j + 1))
            nc.vector.quantize_mx(
                out=e_codes[:, h, columns].bitcast(MXFP8),
                scales=e_scales[:, h, columns],
                in_=e_grouped[part][:].rearrange("p n t -> p (n t)"),
            )

        z_rounded, z_grouped, z_mx = {}, {}, {}

        def z_matmul(s, h):
            codes, scales = x_mx[s]
            z_rounded[(s, h)] = rotating.tile([P, WORD, PAIR], BF16, name="z_rounded", bufs=3, align_bytes=64)
            for i in range(WORD // 2):
                bank = psum.tile([P, 2, PAIR], F32, name="sums_ps", bufs=4)
                for t in (2 * i, 2 * i + 1):
                    m = PASS * h + P * t
                    for g in range(FEATURE_PASSES):
                        nc.tensor.matmul_mx(
                            out=bank[:, t - 2 * i, :],
                            lhsT=comp_codes[:, g, m : m + P].bitcast(MXFP8),
                            lhsT_scale=comp_scales[:, g, m : m + P],
                            rhs=codes[:, g, :].bitcast(MXFP8),
                            rhs_scale=scales[:, g, :],
                            start=(g == 0),
                            stop=(g == FEATURE_PASSES - 1),
                        )
                for t in (2 * i, 2 * i + 1):
                    column = WORD * h + t
                    nc.scalar.activation(
                        out=z_rounded[(s, h)][:, t, :],
                        in_=bank[:, t - 2 * i, :],
                        func=COPY,
                        scale=gain_columns[:, column : column + 1],
                    )

        def z_group(s, h, copy):
            z_grouped[(s, h)] = rotating.tile([P, PAIR, WORD], BF16, name="z_grouped", bufs=4, align_bytes=64)
            copy(
                out=z_grouped[(s, h)][:].rearrange("p (k i) t -> p k t i", i=4),
                in_=z_rounded[(s, h)][:].rearrange("p t (k i) -> p k t i", i=4),
            )

        def z_quantize(s, h):
            codes = rotating.tile([P, PAIR], U32, name="z_codes", bufs=8, align_bytes=64)
            scales = rotating.tile([P, PAIR], U8, name="z_scales", bufs=8, align_bytes=64)
            nc.vector.quantize_mx(
                out=codes[:].bitcast(MXFP8),
                scales=scales[:],
                in_=z_grouped[(s, h)][:].rearrange("p r t -> p (r t)"),
            )
            z_mx[(s, h)] = (codes, scales)

        products = {}

        def y_direct(i, j):
            s, place = divmod(i, 2)
            columns = slice(HALF * j, HALF * (j + 1))
            bank = psum.tile([P, HALF], F32, name="direct_ps", bufs=2)
            for h in range(CHANNEL_PASSES):
                codes, scales = z_mx[(s, h)]
                nc.tensor.matmul_mx(
                    out=bank[:],
                    lhsT=codes[:, P * place : P * (place + 1)].bitcast(MXFP8),
                    lhsT_scale=scales[:, P * place : P * (place + 1)],
                    rhs=e_codes[:, h, columns].bitcast(MXFP8),
                    rhs_scale=e_scales[:, h, columns],
                    start=(h == 0),
                    stop=(h == CHANNEL_PASSES - 1),
                )
            products[(i, j)] = rotating.tile(
                [P, COPIES, HALF], F32, name="product", tag="four_kib", bufs=8, align_bytes=64
            )
            nc.vector.tensor_tensor(
                out=products[(i, j)][:],
                in0=bank[:].unsqueeze(1).to_broadcast([P, COPIES, HALF]),
                in1=copy_gain_sb[:, :, columns],
                op=MULT,
            )

        def add_base(i, j):
            columns = slice(HALF * j, HALF * (j + 1))
            product = products[(i, j)]
            nc.vector.tensor_tensor(out=product[:], in0=product[:], in1=base_rows[i][:, :, columns], op=ADD)
            rows = out[P * i : P * (i + 1), :].rearrange("p (c n) -> p c n", c=COPIES)
            nc.sync.dma_start(out=rows[:, :, columns], in_=product[:])

        turned_products = {}

        def y_transposed(s, j):
            banks = []
            for b in range(BLOCKS):
                if b % 2 == 0:
                    banks.append(psum.tile([P, 2, PAIR], F32, name="sums_ps", bufs=4))
                columns = slice(HALF * j + P * b, HALF * j + P * (b + 1))
                for h in range(CHANNEL_PASSES):
                    codes, scales = z_mx[(s, h)]
                    nc.tensor.matmul_mx(
                        out=banks[b // 2][:, b % 2, :],
                        lhsT=e_codes[:, h, columns].bitcast(MXFP8),
                        lhsT_scale=e_scales[:, h, columns],
                        rhs=codes[:].bitcast(MXFP8),
                        rhs_scale=scales[:],
                        start=(h == 0),
                        stop=(h == CHANNEL_PASSES - 1),
                    )
            turned = rotating.tile([P, COPIES, BLOCKS, PAIR], F32, name="turned", align_bytes=64)
            for c in range(COPIES):
                for b in range(BLOCKS):
                    column = GAIN_COLUMNS + c * (COLUMNS // P) + BLOCKS * j + b
                    nc.scalar.activation(
                        out=turned[:, c, b, :],
                        in_=banks[b // 2][:, b % 2, :],
                        func=COPY,
                        scale=gain_columns[:, column : column + 1],
                    )
            turned_products[(s, j)] = turned

        def turn_back(i, j, c):
            s, place = divmod(i, 2)
            bank = psum.tile([P, BLOCKS, P], F32, name="turned_ps", bufs=2)
            for b in range(BLOCKS):
                nc.tensor.transpose(
                    bank[:, b, :], turned_products[(s, j)][:, c, b, P * place : P * (place + 1)], identity[:]
                )
            total = rotating.tile([P, HALF], F32, name="total", bufs=8, align_bytes=64)
            nc.vector.tensor_tensor(
                out=total[:],
                in0=bank[:].rearrange("p b n -> p (b n)"),
                in1=base_rows[i][:, c, HALF * j : HALF * (j + 1)],
                op=ADD,
            )
            first = COLUMNS * c + HALF * j
            nc.sync.dma_start(out=out[P * i : P * (i + 1), first : first + HALF], in_=total[:])

        load_comp(0)
        load_scales(a_scales_raw, a_scales)
        load_x(0)
        load_codes(a_codes_raw, a_words)
        load_codes(d_codes, d_words)
        load_scales(d_scales_sb, d_scales)
        load_comp(1)
        load_x(1)
        load_comp(2)
        load_x(2)
        load_gains()
        load_x(3)
        for piece in range(3, 7):
            load_comp(piece)
        load_x(4)
        load_comp(7)
        for i in range(5, 8):
            load_x(i)
        nc.sync.dma_start(
            out=copy_gain_sb[:].rearrange("p c n -> p (c n)"),
            in_=copy_gain.rearrange("c n -> (c n)").partition_broadcast(P),
        )
        for i in range(TOKENS // P):
            load_base(i)

        comp_group(0)
        permute_a()
        x_transpose(0)
        comp_quantize(0)
        e_matmul(0, 0)
        e_matmul(0, 1)
        x_transpose(1)
        comp_group(1)
        e_matmul(1, 0)
        comp_quantize(1)
        comp_group(2)
        x_transpose(2)
        e_quantize(0)
        e_matmul(1, 1)
        x_transpose(3)
        e_matmul(2, 0)
        x_quantize(0)
        comp_quantize(2)
        e_matmul(2, 1)
        e_matmul(3, 0)
        x_transpose(4)
        for piece in range(3, 6):
            comp_group(piece)
        for piece in range(3, 6):
            comp_quantize(piece)

        turn_gains()
        comp_group(6)
        z_matmul(0, 0)
        x_transpose(5)
        comp_group(7)
        z_group(0, 0, nc.scalar.copy)
        comp_quantize(6)
        comp_quantize(7)
        e_quantize(1)
        x_quantize(1)
        e_matmul(3, 1)
        x_quantize(2)
        e_quantize(2)
        z_matmul(0, 1)
        x_transpose(6)
        e_quantize(3)
        z_group(0, 1, nc.vector.tensor_copy)
        z_matmul(1, 0)
        z_quantize(0, 0)
        z_quantize(0, 1)

        y_direct(0, 0)
        z_group(1, 0, nc.scalar.copy)
        y_direct(1, 0)
        x_transpose(7)
        add_base(0, 0)
        z_matmul(2, 0)
        x_quantize(3)
        z_quantize(1, 0)
        y_direct(0, 1)
        z_group(2, 0, nc.scalar.copy)
        z_matmul(1, 1)
        z_group(1, 1, nc.scalar.copy)
        add_base(1, 0)
        z_quantize(2, 0)
        add_base(0, 1)
        z_matmul(2, 1)
        z_quantize(1, 1)
        z_group(2, 1, nc.scalar.copy)
        y_direct(1, 1)
        z_matmul(3, 1)
        add_base(1, 1)
        z_group(3, 1, nc.scalar.copy)
        z_quantize(2, 1)
        y_direct(2, 0)
        y_direct(3, 0)

        y_transposed(2, 0)
        add_base(2, 0)
        y_direct(2, 1)
        y_transposed(2, 1)
        y_direct(3, 1)
        turn_back(4, 0, 0)
        z_matmul(3, 0)
        add_base(3, 0)
        turn_back(4, 0, 1)
        turn_back(5, 0, 0)
        z_group(3, 0, nc.scalar.copy)
        z_quantize(3, 1)
        turn_back(5, 0, 1)
        turn_back(4, 1, 0)
        z_quantize(3, 0)
        turn_back(4, 1, 1)
        turn_back(5, 1, 0)
        add_base(2, 1)
        y_transposed(3, 0)
        turn_back(5, 1, 1)
        add_base(3, 1)

        turn_back(6, 0, 0)
        y_transposed(3, 1)
        turn_back(6, 0, 1)
        turn_back(7, 0, 0)
        turn_back(7, 0, 1)
        turn_back(6, 1, 0)
        turn_back(6, 1, 1)
        turn_back(7, 1, 0)
        turn_back(7, 1, 1)
